import numpy as np
import ml_dtypes


def mxq(x, axis, fmt="e4m3"):
    dtype, down = {"e4m3": (ml_dtypes.float8_e4m3fn, 7), "e5m2": (ml_dtypes.float8_e5m2, 14)}[fmt]
    v = np.moveaxis(np.asarray(x, np.float32).astype(ml_dtypes.bfloat16).astype(np.float64), axis, -1)
    blocks = v.reshape(v.shape[:-1] + (-1, 32))
    amax = np.abs(blocks).max(-1, keepdims=True)
    byte = np.maximum(np.where(amax > 0, np.frexp(amax)[1] - 1 + 127, 0) - down, 1)
    scale = np.exp2(byte - 127.0)
    codes = (blocks / scale).astype(np.float32).astype(dtype).astype(np.float64)
    return np.moveaxis((codes * scale).reshape(v.shape), -1, axis)


WIDE = False


def mx_kscale(k):
    if not WIDE:
        return np.ones(k)
    levels = np.array([10, -10, 5, -5, 0])
    if k % 512:
        return np.exp2(np.random.permutation(np.resize(levels, k // 32))).repeat(32)
    a = np.empty((k // 512, 16))
    for p in range(k // 512):
        a[p, :8] = np.random.permutation(np.resize(levels, 8))
        for g in range(8):
            far = levels[np.abs(levels - a[p, g]) >= 10]
            a[p, g + 8] = far[np.random.randint(len(far))]
    return np.exp2(a.ravel()).repeat(32)


def f64(x):
    return np.asarray(x).astype(np.float64)


def striped(idx):
    return np.tile(np.asarray(idx).reshape(-1, 16).T, (8, 1)).astype(np.uint16)


def unstriped(offs):
    return offs[:16].T.reshape(-1).astype(np.int64)


E2M1 = np.array([0.0, 0.5, 1.0, 1.5, 2.0, 3.0, 4.0, 6.0, -0.0, -0.5, -1.0, -1.5, -2.0, -3.0, -4.0, -6.0])


def pack_weight(w, fmt):
    k, n = w.shape
    w = f64(np.asarray(w, np.float32).astype(ml_dtypes.bfloat16)).reshape(k // 32, 32, n)
    amax = np.abs(w).max(1)
    if fmt == "e4m3":
        byte = np.frexp(amax)[1] - 1 + 127 - 7
    else:
        mant, ex = np.frexp(amax / 6.0)
        byte = np.where(mant > 0.5, ex, ex - 1) + 127
    byte = np.clip(np.where(amax > 0, byte, 1), 1, 254)
    scaled = (w * np.exp2(127.0 - byte)[:, None, :]).reshape(k, n).astype(np.float32)
    by_word = np.ascontiguousarray(scaled.reshape(k // 512, 128, 4, n).transpose(0, 1, 3, 2))
    if fmt == "e4m3":
        words = by_word.astype(ml_dtypes.float8_e4m3fn).view(np.uint8)
    else:
        c = by_word.astype(ml_dtypes.float4_e2m1fn).view(np.uint8) & 0xF
        words = (c[..., 0::2] | (c[..., 1::2] << 4)).reshape(k // 512, 128, 2 * n)
    return np.ascontiguousarray(words), np.ascontiguousarray(byte.astype(np.uint8).reshape(k // 512, 16, n))


def unpack_weight(words, scales, fmt):
    g, _, n = scales.shape
    words = np.ascontiguousarray(words).reshape(g, 128, n, -1)
    if fmt == "e4m3":
        vals = words.view(ml_dtypes.float8_e4m3fn).astype(np.float64)
    else:
        nib = np.empty((g, 128, n, 4), np.uint8)
        nib[..., 0::2] = words & 0xF
        nib[..., 1::2] = words >> 4
        vals = E2M1[nib]
    vals = vals * np.repeat(np.exp2(scales.astype(np.float64) - 127.0), 8, axis=1)[..., None]
    return vals.transpose(0, 1, 3, 2).reshape(g * 512, n)


K, T, R, U, I, F, M = 512, 2048, 1024, 2048, 512, 512, 256


def setup_inputs():
    n = np.random.standard_normal
    idx = np.random.permutation(T)[:I]
    idx2 = np.random.permutation(U)[:I]
    fk = mx_kscale(K)
    fr = mx_kscale(R)
    ff = mx_kscale(F)
    quesp = pack_weight(n((K, T)) / fk[:, None], "e4m3")
    imgp = pack_weight(n((R, U)) / fr[:, None], "e2m1")
    return {
        "ques_words": quesp[0],
        "ques_scales": quesp[1],
        "img_words": imgp[0],
        "img_scales": imgp[1],
        "wq": (n((K, F)) * 1 / np.sqrt(K) * fk[:, None]).astype(np.float32),
        "wi": (n((R, F)) * 1 / np.sqrt(R) * fr[:, None]).astype(np.float32),
        "gain": (np.random.uniform(0.5, 2.0, (F, 1)) * ff[:, None]).astype(np.float32),
        "wo": (n((F, M)) * 2 / np.sqrt(F) / ff[:, None]).astype(np.float32),
        "offs": striped(idx),
        "offs2": striped(idx2),
    }


def reference(ques_words, ques_scales, img_words, img_scales, wq, wi, gain, wo, offs, offs2):
    idx = unstriped(offs)
    idx2 = unstriped(offs2)
    quesu = unpack_weight(ques_words, ques_scales, "e4m3")
    imgu = unpack_weight(img_words, img_scales, "e2m1")
    wqq = mxq(f64(wq), 0, "e4m3")
    quesidxg = quesu[:, idx]
    z = wqq.T @ quesidxg
    wiq = mxq(f64(wi), 0, "e4m3")
    imgidx2g = imgu[:, idx2]
    v = wiq.T @ imgidx2g
    x = np.tanh(z) * np.tanh(v) * f64(gain)
    woq = mxq(f64(wo), 0, "e4m3")
    xq = mxq(x, 0, "e4m3")
    y = woq.T @ xq
    return y

@@ -1,0 +1,209 @@
+from contextlib import ExitStack
+
+import concourse.mybir as mybir
+
+K, T, R, U, I, F, M = 512, 2048, 1024, 2048, 512, 512, 256
+FLOPS = 2 * I * (K * F + R * F + F * M)
+
+F32 = mybir.dt.float32
+BF16 = mybir.dt.bfloat16
+I32 = mybir.dt.int32
+U32 = mybir.dt.uint32
+U16 = mybir.dt.uint16
+U8 = mybir.dt.uint8
+FP8X4 = mybir.dt.float8_e4m3fn_x4
+FP4X4 = mybir.dt.float4_e2m1fn_x4
+TANH = mybir.ActivationFunctionType.Tanh
+MULT = mybir.AluOpType.mult
+
+P = 128
+PACK = 4
+K_PASS = P * PACK
+QUAD = 32
+QUADS = P // QUAD
+HALF = F // 2
+CHUNK = 128
+CHUNKS = I // CHUNK
+GATHER = 256
+QUES_ROW = 8
+SHIFTED = 112
+
+
+def tile_attend_bilinearfuse_kernel(
+    tc, ques_words, ques_scales, img_words, img_scales, wq, wi, gain, wo, offs, offs2, out
+):
+    nc = tc.nc
+    with ExitStack() as ctx:
+        keep = ctx.enter_context(tc.tile_pool(name="keep", bufs=1))
+        psum = ctx.enter_context(tc.psum_pool(name="psum", bufs=1))
+
+        def sb(name, shape, dtype):
+            return keep.tile(shape, dtype, name=name, align_bytes=64)
+
+        ques_list = keep.tile([P, I // 16], U16, name="ques_list")
+        img_list = keep.tile([P, I // 16], U16, name="img_list")
+
+        img_scale_table = sb("img_scale_table", [P, U], U8)
+        ques_scale_table = sb("ques_scale_table", [P, T], U8)
+        img_plane1 = sb("img_plane1", [P, I], U8)
+        warm = sb("warm", [P, 8], F32)
+        warm_out = sb("warm_out", [P, 8], F32)
+        nc.gpsimd.memset(img_scale_table[:].bitcast(I32), 0)
+        nc.vector.memset(warm[:], 0.0)
+        nc.scalar.activation(warm_out[:], warm[:], TANH)
+        nc.vector.memset(ques_scale_table[:].bitcast(I32), 0)
+        nc.vector.memset(img_plane1[:].bitcast(I32), 0)
+
+        for q in range(QUADS):
+            nc.gpsimd.dma_start(
+                out=img_scale_table[QUAD * q : QUAD * q + 8, :].bitcast(I32),
+                in_=img_scales[:, 4 * q : 4 * q + 4, :].bitcast(I32),
+            )
+
+        for q in range(QUADS):
+            nc.scalar.dma_start(
+                out=ques_scale_table[QUAD * q + QUES_ROW : QUAD * q + QUES_ROW + 4, :].bitcast(I32),
+                in_=ques_scales[0, 4 * q : 4 * q + 4, :].bitcast(I32),
+            )
+
+        def load_halves(name, rows):
+            halves = []
+            for h in range(2):
+                raw = sb(f"{name}_raw{h}", [P, PACK, HALF], F32)
+                nc.sync.dma_start(
+                    out=raw[:],
+                    in_=rows.rearrange("(p j) c -> p j c", j=PACK)[:, :, h * HALF : (h + 1) * HALF],
+                )
+                halves.append(raw)
+            return halves
+
+        wi_raw = [load_halves("wi0", wi[0:K_PASS, :])]
+        nc.sync.dma_start(img_list[:], offs2)
+        nc.sync.dma_start(ques_list[:], offs)
+        wi_raw.append(load_halves("wi1", wi[K_PASS : 2 * K_PASS, :]))
+        img_tables = []
+        for z in range(2):
+            table = sb(f"img_table{z}", [P, U], U16)
+            nc.sync.dma_start(out=table[:].bitcast(I32), in_=img_words[z].bitcast(I32))
+            img_tables.append(table)
+        gain_sb = sb("gain_sb", [P, PACK], F32)
+        nc.sync.dma_start(out=gain_sb[:], in_=gain.rearrange("(p t) o -> p (t o)", t=PACK))
+        wq_raw = load_halves("wq", wq)
+        ques_table = sb("ques_table", [P, T], U32)
+        nc.sync.dma_start(
+            out=ques_table[:].bitcast(I32),
+            in_=ques_words[0].rearrange("p n t -> p (n t)").bitcast(I32),
+        )
+        wo_raw = sb("wo_raw", [P, PACK, M], F32)
+        nc.sync.dma_start(out=wo_raw[:], in_=wo.rearrange("(p j) m -> p j m", j=PACK))
+
+        def deal(copies, grouped, halves):
+            per = HALF // PACK
+            for h, raw in enumerate(halves):
+                copies[h](
+                    out=grouped[:, :, h * per : (h + 1) * per, :].rearrange("p t m j -> p m j t"),
+                    in_=raw[:].rearrange("p j (m t) -> p m j t", t=PACK),
+                )
+
+        def quantise(name, values, width):
+            codes = sb(f"{name}_codes", [P, width], U32)
+            plane = sb(f"{name}_plane", [P, width], U8)
+            nc.vector.quantize_mx(out=codes[:].bitcast(FP8X4), scales=plane[:], in_=values)
+            return codes, plane
+
+        ques_plane = sb("ques_plane", [P, I], U8)
+        nc.vector.tensor_copy(ques_plane[:], ques_scale_table[:].indirect(ques_list[:]))
+        img_plane0 = sb("img_plane0", [P, I], U8)
+        nc.vector.tensor_copy(img_plane0[:], img_scale_table[:].indirect(img_list[:]))
+        nc.gpsimd.dma_start(
+            out=img_plane1[0:SHIFTED, :].bitcast(I32),
+            in_=img_plane0[4 : 4 + SHIFTED, :].bitcast(I32),
+        )
+        img_planes = [img_plane0, img_plane1]
+        wi_q = []
+        for z in range(2):
+            grouped = sb(f"wi{z}_grouped", [P, PACK, P, PACK], BF16)
+            deal([nc.scalar.copy] * 2, grouped, wi_raw[z])
+            wi_q.append(quantise(f"wi{z}", grouped[:].rearrange("p t m j -> p (t m j)"), F))
+        v_banks = [psum.tile([P, I], F32, name=f"v_bank{t}", tag=f"bank{t}") for t in range(PACK)]
+        for z in range(2):
+            picked = sb(f"img_picked{z}", [P, I], U16)
+            nc.vector.tensor_copy(picked[:], img_tables[z][:].indirect(img_list[:]))
+            codes, plane = wi_q[z]
+            for t in range(PACK):
+                cols = slice(t * P, (t + 1) * P)
+                nc.tensor.matmul_mx(
+                    out=v_banks[t][:],
+                    lhsT=codes[:, cols].bitcast(FP8X4),
+                    lhsT_scale=plane[:, cols],
+                    rhs=picked[:].bitcast(FP4X4),
+                    rhs_scale=img_planes[z][:],
+                    start=(z == 0),
+                    stop=(z == 1),
+                )
+        wq_grouped = sb("wq_grouped", [P, PACK, P, PACK], BF16)
+        deal([nc.scalar.copy, nc.vector.tensor_copy], wq_grouped, wq_raw)
+        tv_gain = sb("tv_gain", [P, PACK, I], F32)
+        for t in range(PACK):
+            tv = sb(f"tv{t}", [P, I], F32)
+            nc.scalar.activation(tv[:], v_banks[t][:], TANH)
+            nc.vector.tensor_scalar(tv_gain[:, t, :], tv[:], gain_sb[:, t : t + 1], None, MULT)
+        wq_codes, wq_plane = quantise("wq", wq_grouped[:].rearrange("p t m j -> p (t m j)"), F)
+
+        ques_picked = []
+        for g in range(I // GATHER):
+            picked = sb(f"ques_picked{g}", [P, GATHER], U32)
+            columns = slice(g * GATHER // 16, (g + 1) * GATHER // 16)
+            nc.vector.tensor_copy(picked[:], ques_table[:].indirect(ques_list[:, columns]))
+            ques_picked.append(picked)
+        wo_grouped = sb("wo_grouped", [P, M, PACK], BF16)
+        nc.vector.tensor_copy(
+            out=wo_grouped[:].rearrange("p (c e) j -> p c j e", e=2),
+            in_=wo_raw[:].rearrange("p j (c e) -> p c j e", e=2),
+        )
+        tz = []
+        for c in range(CHUNKS):
+            bank = psum.tile([P, PACK, CHUNK], F32, name=f"z_bank{c}", tag=f"bank{PACK + c}")
+            g, first = divmod(c * CHUNK, GATHER)
+            for t in range(PACK):
+                cols = slice(t * P, (t + 1) * P)
+                nc.tensor.matmul_mx(
+                    out=bank[:, t, :],
+                    lhsT=wq_codes[:, cols].bitcast(FP8X4),
+                    lhsT_scale=wq_plane[:, cols],
+                    rhs=ques_picked[g][:, first : first + CHUNK].bitcast(FP8X4),
+                    rhs_scale=ques_plane[QUES_ROW:P, c * CHUNK : (c + 1) * CHUNK],
+                    start=True,
+                    stop=True,
+                )
+            tanh_z = sb(f"tz{c}", [P, PACK, CHUNK], F32)
+            nc.scalar.activation(tanh_z[:], bank[:], TANH)
+            tz.append(tanh_z)
+        wo_codes, wo_plane = quantise("wo", wo_grouped[:].rearrange("p m j -> p (m j)"), M)
+
+        out_view = out.rearrange("(h p) i -> p h i", p=P)
+        for c in range(CHUNKS):
+            pairs = slice(c * CHUNK, (c + 1) * CHUNK)
+            x = sb(f"x{c}", [P, CHUNK, PACK], BF16)
+            nc.vector.tensor_tensor(
+                x[:].rearrange("p (c e) t -> p c t e", e=2),
+                tz[c][:].rearrange("p t (c e) -> p c t e", e=2),
+                tv_gain[:, :, pairs].rearrange("p t (c e) -> p c t e", e=2),
+                MULT,
+            )
+            x_codes, x_plane = quantise(f"x{c}", x[:].rearrange("p i t -> p (i t)"), CHUNK)
+            bank = psum.tile([P, M // P, CHUNK], F32, name=f"out_bank{c}", tag=f"bank{c}")
+            for h in range(M // P):
+                cols = slice(h * P, (h + 1) * P)
+                nc.tensor.matmul_mx(
+                    out=bank[:, h, :],
+                    lhsT=wo_codes[:, cols].bitcast(FP8X4),
+                    lhsT_scale=wo_plane[:, cols],
+                    rhs=x_codes[:].bitcast(FP8X4),
+                    rhs_scale=x_plane[:],
+                    start=True,
+                    stop=True,
+                )
+            result = sb(f"result{c}", [P, M // P, CHUNK], F32)
+            nc.scalar.copy(out=result[:], in_=bank[:])
+            nc.sync.dma_start(out=out_view[:, :, pairs], in_=result[:])

@@ -27,6 +27,14 @@ CHUNKS = I // CHUNK
 GATHER = 256
 QUES_ROW = 8
 SHIFTED = 112
+SHARED = {
+    "img_scale_table": 0, "wi0_codes": 0,
+    "wi0_grouped": 2048, "img_picked0": 2048,
+    "img_table0": 6144, "img_picked1": 6144,
+    "ques_plane": 10240, "img_table1": 10240, "wq_grouped": 10752,
+    "ques_picked0": 10752, "ques_picked1": 11776,
+    "ques_table": 14848, "wo_grouped": 14848,
+}
 
 
 def tile_attend_bilinearfuse_kernel(
@@ -35,9 +43,12 @@ def tile_attend_bilinearfuse_kernel(
     nc = tc.nc
     with ExitStack() as ctx:
         keep = ctx.enter_context(tc.tile_pool(name="keep", bufs=1))
+        shared = ctx.enter_context(tc.tile_pool(name="shared", bufs=1))
         psum = ctx.enter_context(tc.psum_pool(name="psum", bufs=1))
 
         def sb(name, shape, dtype):
+            if name in SHARED:
+                return shared.tile(shape, dtype, name=name, offset=SHARED[name], align_bytes=64)
             return keep.tile(shape, dtype, name=name, align_bytes=64)
 
         ques_list = keep.tile([P, I // 16], U16, name="ques_list")
@@ -59,28 +70,21 @@ def tile_attend_bilinearfuse_kernel(
                 out=img_scale_table[QUAD * q : QUAD * q + 8, :].bitcast(I32),
                 in_=img_scales[:, 4 * q : 4 * q + 4, :].bitcast(I32),
             )
-
         for q in range(QUADS):
-            nc.scalar.dma_start(
+            nc.gpsimd.dma_start(
                 out=ques_scale_table[QUAD * q + QUES_ROW : QUAD * q + QUES_ROW + 4, :].bitcast(I32),
                 in_=ques_scales[0, 4 * q : 4 * q + 4, :].bitcast(I32),
             )
 
-        def load_halves(name, rows):
-            halves = []
-            for h in range(2):
-                raw = sb(f"{name}_raw{h}", [P, PACK, HALF], F32)
-                nc.sync.dma_start(
-                    out=raw[:],
-                    in_=rows.rearrange("(p j) c -> p j c", j=PACK)[:, :, h * HALF : (h + 1) * HALF],
-                )
-                halves.append(raw)
-            return halves
+        def load_rows(name, rows):
+            raw = sb(name, [P, PACK, rows.shape[1]], F32)
+            nc.sync.dma_start(out=raw[:], in_=rows.rearrange("(p j) c -> p j c", j=PACK))
+            return raw
 
-        wi_raw = [load_halves("wi0", wi[0:K_PASS, :])]
+        wi_raw = [load_rows("wi0_raw", wi[0:K_PASS, :])]
         nc.sync.dma_start(img_list[:], offs2)
         nc.sync.dma_start(ques_list[:], offs)
-        wi_raw.append(load_halves("wi1", wi[K_PASS : 2 * K_PASS, :]))
+        wi_raw.append(load_rows("wi1_raw", wi[K_PASS : 2 * K_PASS, :]))
         img_tables = []
         for z in range(2):
             table = sb(f"img_table{z}", [P, U], U16)
@@ -88,21 +92,22 @@ def tile_attend_bilinearfuse_kernel(
             img_tables.append(table)
         gain_sb = sb("gain_sb", [P, PACK], F32)
         nc.sync.dma_start(out=gain_sb[:], in_=gain.rearrange("(p t) o -> p (t o)", t=PACK))
-        wq_raw = load_halves("wq", wq)
+        wq_raw = load_rows("wq_raw", wq)
         ques_table = sb("ques_table", [P, T], U32)
         nc.sync.dma_start(
             out=ques_table[:].bitcast(I32),
             in_=ques_words[0].rearrange("p n t -> p (n t)").bitcast(I32),
         )
-        wo_raw = sb("wo_raw", [P, PACK, M], F32)
-        nc.sync.dma_start(out=wo_raw[:], in_=wo.rearrange("(p j) m -> p j m", j=PACK))
+        wo_raw = load_rows("wo_raw", wo)
 
-        def deal(copies, grouped, halves):
-            per = HALF // PACK
-            for h, raw in enumerate(halves):
-                copies[h](
+        def deal(copies, grouped, raw):
+            per = P // len(copies)
+            for h, copy_part in enumerate(copies):
+                copy_part(
                     out=grouped[:, :, h * per : (h + 1) * per, :].rearrange("p t m j -> p m j t"),
-                    in_=raw[:].rearrange("p j (m t) -> p m j t", t=PACK),
+                    in_=raw[:, :, h * per * PACK : (h + 1) * per * PACK].rearrange(
+                        "p j (m t) -> p m j t", t=PACK
+                    ),
                 )
 
         def quantise(name, values, width):
@@ -111,8 +116,6 @@ def tile_attend_bilinearfuse_kernel(
             nc.vector.quantize_mx(out=codes[:].bitcast(FP8X4), scales=plane[:], in_=values)
             return codes, plane
 
-        ques_plane = sb("ques_plane", [P, I], U8)
-        nc.vector.tensor_copy(ques_plane[:], ques_scale_table[:].indirect(ques_list[:]))
         img_plane0 = sb("img_plane0", [P, I], U8)
         nc.vector.tensor_copy(img_plane0[:], img_scale_table[:].indirect(img_list[:]))
         nc.gpsimd.dma_start(
@@ -120,16 +123,13 @@ def tile_attend_bilinearfuse_kernel(
             in_=img_plane0[4 : 4 + SHIFTED, :].bitcast(I32),
         )
         img_planes = [img_plane0, img_plane1]
-        wi_q = []
-        for z in range(2):
-            grouped = sb(f"wi{z}_grouped", [P, PACK, P, PACK], BF16)
-            deal([nc.scalar.copy] * 2, grouped, wi_raw[z])
-            wi_q.append(quantise(f"wi{z}", grouped[:].rearrange("p t m j -> p (t m j)"), F))
         v_banks = [psum.tile([P, I], F32, name=f"v_bank{t}", tag=f"bank{t}") for t in range(PACK)]
         for z in range(2):
+            grouped = sb(f"wi{z}_grouped", [P, PACK, P, PACK], BF16)
+            deal([nc.scalar.copy], grouped, wi_raw[z])
+            codes, plane = quantise(f"wi{z}", grouped[:].rearrange("p t m j -> p (t m j)"), F)
             picked = sb(f"img_picked{z}", [P, I], U16)
             nc.vector.tensor_copy(picked[:], img_tables[z][:].indirect(img_list[:]))
-            codes, plane = wi_q[z]
             for t in range(PACK):
                 cols = slice(t * P, (t + 1) * P)
                 nc.tensor.matmul_mx(
@@ -141,23 +141,26 @@ def tile_attend_bilinearfuse_kernel(
                     start=(z == 0),
                     stop=(z == 1),
                 )
+
+        ques_plane = sb("ques_plane", [P, I], U8)
+        nc.vector.tensor_copy(ques_plane[:], ques_scale_table[:].indirect(ques_list[:]))
         wq_grouped = sb("wq_grouped", [P, PACK, P, PACK], BF16)
         deal([nc.scalar.copy, nc.vector.tensor_copy], wq_grouped, wq_raw)
-        tv_gain = sb("tv_gain", [P, PACK, I], F32)
-        for t in range(PACK):
-            tv = sb(f"tv{t}", [P, I], F32)
-            nc.scalar.activation(tv[:], v_banks[t][:], TANH)
-            nc.vector.tensor_scalar(tv_gain[:, t, :], tv[:], gain_sb[:, t : t + 1], None, MULT)
         wq_codes, wq_plane = quantise("wq", wq_grouped[:].rearrange("p t m j -> p (t m j)"), F)
-
         ques_picked = []
         for g in range(I // GATHER):
             picked = sb(f"ques_picked{g}", [P, GATHER], U32)
             columns = slice(g * GATHER // 16, (g + 1) * GATHER // 16)
             nc.vector.tensor_copy(picked[:], ques_table[:].indirect(ques_list[:, columns]))
             ques_picked.append(picked)
+
+        tv_gain = sb("tv_gain", [P, PACK, I], F32)
+        for t in range(PACK):
+            tv = sb(f"tv{t}", [P, I], F32)
+            nc.scalar.activation(tv[:], v_banks[t][:], TANH)
+            nc.vector.tensor_scalar(tv_gain[:, t, :], tv[:], gain_sb[:, t : t + 1], None, MULT)
         wo_grouped = sb("wo_grouped", [P, M, PACK], BF16)
-        nc.vector.tensor_copy(
+        nc.scalar.copy(
             out=wo_grouped[:].rearrange("p (c e) j -> p c j e", e=2),
             in_=wo_raw[:].rearrange("p j (c e) -> p c j e", e=2),
         )

@@ -26,14 +26,13 @@ CHUNK = 128
 CHUNKS = I // CHUNK
 GATHER = 256
 QUES_ROW = 8
-SHIFTED = 112
+SCALAR_SHARE = 48
 SHARED = {
-    "img_scale_table": 0, "wi0_codes": 0,
-    "wi0_grouped": 2048, "img_picked0": 2048,
-    "img_table0": 6144, "img_picked1": 6144,
-    "ques_plane": 10240, "img_table1": 10240, "wq_grouped": 10752,
-    "ques_picked0": 10752, "ques_picked1": 11776,
-    "ques_table": 14848, "wo_grouped": 14848,
+    "img_scale_table": 0, "img_picked1": 0,
+    "wi0_grouped": 4096, "wi1_grouped": 4096, "wq_grouped": 4096,
+    "ques_picked0": 4096, "ques_picked1": 5120,
+    "wq_raw": 8192, "wo_grouped": 8192,
+    "ques_table": 16384, "tv_gain": 16384,
 }
 
 
@@ -54,44 +53,44 @@ def tile_attend_bilinearfuse_kernel(
         ques_list = keep.tile([P, I // 16], U16, name="ques_list")
         img_list = keep.tile([P, I // 16], U16, name="img_list")
 
-        img_scale_table = sb("img_scale_table", [P, U], U8)
+        img_scale_table = sb("img_scale_table", [P, 2, U], U8)
         ques_scale_table = sb("ques_scale_table", [P, T], U8)
-        img_plane1 = sb("img_plane1", [P, I], U8)
         warm = sb("warm", [P, 8], F32)
         warm_out = sb("warm_out", [P, 8], F32)
-        nc.gpsimd.memset(img_scale_table[:].bitcast(I32), 0)
+        nc.gpsimd.memset(img_scale_table[:, 0, :].bitcast(I32), 0)
+        nc.vector.memset(img_scale_table[:, 1, :].bitcast(I32), 0)
         nc.vector.memset(warm[:], 0.0)
         nc.scalar.activation(warm_out[:], warm[:], TANH)
         nc.vector.memset(ques_scale_table[:].bitcast(I32), 0)
-        nc.vector.memset(img_plane1[:].bitcast(I32), 0)
-
-        for q in range(QUADS):
-            nc.gpsimd.dma_start(
-                out=img_scale_table[QUAD * q : QUAD * q + 8, :].bitcast(I32),
-                in_=img_scales[:, 4 * q : 4 * q + 4, :].bitcast(I32),
-            )
-        for q in range(QUADS):
-            nc.gpsimd.dma_start(
-                out=ques_scale_table[QUAD * q + QUES_ROW : QUAD * q + QUES_ROW + 4, :].bitcast(I32),
-                in_=ques_scales[0, 4 * q : 4 * q + 4, :].bitcast(I32),
-            )
 
         def load_rows(name, rows):
             raw = sb(name, [P, PACK, rows.shape[1]], F32)
             nc.sync.dma_start(out=raw[:], in_=rows.rearrange("(p j) c -> p j c", j=PACK))
             return raw
 
-        wi_raw = [load_rows("wi0_raw", wi[0:K_PASS, :])]
-        nc.sync.dma_start(img_list[:], offs2)
-        nc.sync.dma_start(ques_list[:], offs)
-        wi_raw.append(load_rows("wi1_raw", wi[K_PASS : 2 * K_PASS, :]))
-        img_tables = []
-        for z in range(2):
+        def load_img_table(z):
             table = sb(f"img_table{z}", [P, U], U16)
             nc.sync.dma_start(out=table[:].bitcast(I32), in_=img_words[z].bitcast(I32))
-            img_tables.append(table)
+            return table
+
+        nc.sync.dma_start(img_list[:], offs2)
+        nc.sync.dma_start(ques_list[:], offs)
         gain_sb = sb("gain_sb", [P, PACK], F32)
         nc.sync.dma_start(out=gain_sb[:], in_=gain.rearrange("(p t) o -> p (t o)", t=PACK))
+        img_tables = [load_img_table(0)]
+        for r in range(4):
+            nc.sync.dma_start(
+                out=img_scale_table[r:P:QUAD, :, :].bitcast(I32),
+                in_=img_scales[:, r:16:4, :].rearrange("z q c -> q z c").bitcast(I32),
+            )
+        wi_raw = [load_rows("wi0_raw", wi[0:K_PASS, :])]
+        img_tables.append(load_img_table(1))
+        for r in range(4):
+            nc.sync.dma_start(
+                out=ques_scale_table[QUES_ROW + r : P : QUAD, :].bitcast(I32),
+                in_=ques_scales[0, r:16:4, :].bitcast(I32),
+            )
+        wi_raw.append(load_rows("wi1_raw", wi[K_PASS : 2 * K_PASS, :]))
         wq_raw = load_rows("wq_raw", wq)
         ques_table = sb("ques_table", [P, T], U32)
         nc.sync.dma_start(
@@ -100,15 +99,16 @@ def tile_attend_bilinearfuse_kernel(
         )
         wo_raw = load_rows("wo_raw", wo)
 
-        def deal(copies, grouped, raw):
-            per = P // len(copies)
-            for h, copy_part in enumerate(copies):
-                copy_part(
-                    out=grouped[:, :, h * per : (h + 1) * per, :].rearrange("p t m j -> p m j t"),
-                    in_=raw[:, :, h * per * PACK : (h + 1) * per * PACK].rearrange(
-                        "p j (m t) -> p m j t", t=PACK
-                    ),
-                )
+        def deal(name, raw, scalar_share):
+            grouped = sb(f"{name}_grouped", [P, PACK, P, PACK], BF16)
+            parts = [(nc.scalar.copy, 0, scalar_share), (nc.vector.tensor_copy, scalar_share, P)]
+            for copy_part, lo, hi in parts:
+                if lo < hi:
+                    copy_part(
+                        out=grouped[:, :, lo:hi, :].rearrange("p t m j -> p m j t"),
+                        in_=raw[:, :, lo * PACK : hi * PACK].rearrange("p j (m t) -> p m j t", t=PACK),
+                    )
+            return grouped[:].rearrange("p t m j -> p (t m j)")
 
         def quantise(name, values, width):
             codes = sb(f"{name}_codes", [P, width], U32)
@@ -116,43 +116,41 @@ def tile_attend_bilinearfuse_kernel(
             nc.vector.quantize_mx(out=codes[:].bitcast(FP8X4), scales=plane[:], in_=values)
             return codes, plane
 
-        img_plane0 = sb("img_plane0", [P, I], U8)
-        nc.vector.tensor_copy(img_plane0[:], img_scale_table[:].indirect(img_list[:]))
-        nc.gpsimd.dma_start(
-            out=img_plane1[0:SHIFTED, :].bitcast(I32),
-            in_=img_plane0[4 : 4 + SHIFTED, :].bitcast(I32),
-        )
-        img_planes = [img_plane0, img_plane1]
+        def gather(name, window, offsets, width, dtype):
+            picked = sb(name, [P, width], dtype)
+            nc.vector.tensor_copy(picked[:], window.indirect(offsets))
+            return picked
+
+        img_picked = [gather("img_picked0", img_tables[0][:], img_list[:], I, U16)]
+        img_planes = [
+            gather(f"img_plane{z}", img_scale_table[:, z, :], img_list[:], I, U8) for z in range(2)
+        ]
+        img_picked.append(gather("img_picked1", img_tables[1][:], img_list[:], I, U16))
+        ques_plane = gather("ques_plane", ques_scale_table[:], ques_list[:], I, U8)
+
         v_banks = [psum.tile([P, I], F32, name=f"v_bank{t}", tag=f"bank{t}") for t in range(PACK)]
         for z in range(2):
-            grouped = sb(f"wi{z}_grouped", [P, PACK, P, PACK], BF16)
-            deal([nc.scalar.copy], grouped, wi_raw[z])
-            codes, plane = quantise(f"wi{z}", grouped[:].rearrange("p t m j -> p (t m j)"), F)
-            picked = sb(f"img_picked{z}", [P, I], U16)
-            nc.vector.tensor_copy(picked[:], img_tables[z][:].indirect(img_list[:]))
+            share = P if z == 0 else SCALAR_SHARE
+            codes, plane = quantise(f"wi{z}", deal(f"wi{z}", wi_raw[z], share), F)
             for t in range(PACK):
                 cols = slice(t * P, (t + 1) * P)
                 nc.tensor.matmul_mx(
                     out=v_banks[t][:],
                     lhsT=codes[:, cols].bitcast(FP8X4),
                     lhsT_scale=plane[:, cols],
-                    rhs=picked[:].bitcast(FP4X4),
+                    rhs=img_picked[z][:].bitcast(FP4X4),
                     rhs_scale=img_planes[z][:],
                     start=(z == 0),
                     stop=(z == 1),
                 )
+        wq_codes, wq_plane = quantise("wq", deal("wq", wq_raw, SCALAR_SHARE), F)
 
-        ques_plane = sb("ques_plane", [P, I], U8)
-        nc.vector.tensor_copy(ques_plane[:], ques_scale_table[:].indirect(ques_list[:]))
-        wq_grouped = sb("wq_grouped", [P, PACK, P, PACK], BF16)
-        deal([nc.scalar.copy, nc.vector.tensor_copy], wq_grouped, wq_raw)
-        wq_codes, wq_plane = quantise("wq", wq_grouped[:].rearrange("p t m j -> p (t m j)"), F)
         ques_picked = []
         for g in range(I // GATHER):
-            picked = sb(f"ques_picked{g}", [P, GATHER], U32)
             columns = slice(g * GATHER // 16, (g + 1) * GATHER // 16)
-            nc.vector.tensor_copy(picked[:], ques_table[:].indirect(ques_list[:, columns]))
-            ques_picked.append(picked)
+            ques_picked.append(
+                gather(f"ques_picked{g}", ques_table[:], ques_list[:, columns], GATHER, U32)
+            )
 
         tv_gain = sb("tv_gain", [P, PACK, I], F32)
         for t in range(PACK):

@@ -14,25 +14,28 @@ U8 = mybir.dt.uint8
 FP8X4 = mybir.dt.float8_e4m3fn_x4
 FP4X4 = mybir.dt.float4_e2m1fn_x4
 TANH = mybir.ActivationFunctionType.Tanh
+COPY = mybir.ActivationFunctionType.Copy
 MULT = mybir.AluOpType.mult
 
 P = 128
 PACK = 4
 K_PASS = P * PACK
 QUAD = 32
-QUADS = P // QUAD
-HALF = F // 2
 CHUNK = 128
 CHUNKS = I // CHUNK
 GATHER = 256
 QUES_ROW = 8
-SCALAR_SHARE = 48
+PASS_ROW = 16
+FIRST_SHARE = 104
+SCALAR_SHARE = 60
+VECTOR_GAINS = 2
 SHARED = {
-    "img_scale_table": 0, "img_picked1": 0,
-    "wi0_grouped": 4096, "wi1_grouped": 4096, "wq_grouped": 4096,
-    "ques_picked0": 4096, "ques_picked1": 5120,
-    "wq_raw": 8192, "wo_grouped": 8192,
-    "ques_table": 16384, "tv_gain": 16384,
+    "wq_raw": 0, "img_scale_table": 0, "tv_gain": 0,
+    "wi0_raw": 8192, "ques_table": 8192, "wo_grouped": 8192,
+    "wi0_grouped": 16384, "wi1_grouped": 16384, "wq_grouped": 16384, "ques_picked0": 16384,
+    "wi1_raw": 20480, "wo_raw": 20480,
+    "tv3": 28672, "tz0": 28672,
+    "ques_scale_table": 30720, "wi0_codes": 30720,
 }
 
 
@@ -53,15 +56,16 @@ def tile_attend_bilinearfuse_kernel(
         ques_list = keep.tile([P, I // 16], U16, name="ques_list")
         img_list = keep.tile([P, I // 16], U16, name="img_list")
 
-        img_scale_table = sb("img_scale_table", [P, 2, U], U8)
+        img_scale_table = sb("img_scale_table", [P, U], U8)
         ques_scale_table = sb("ques_scale_table", [P, T], U8)
+        img_plane1 = sb("img_plane1", [P, I], U8)
         warm = sb("warm", [P, 8], F32)
         warm_out = sb("warm_out", [P, 8], F32)
-        nc.gpsimd.memset(img_scale_table[:, 0, :].bitcast(I32), 0)
-        nc.vector.memset(img_scale_table[:, 1, :].bitcast(I32), 0)
+        nc.vector.memset(img_scale_table[:].bitcast(I32), 0)
         nc.vector.memset(warm[:], 0.0)
         nc.scalar.activation(warm_out[:], warm[:], TANH)
         nc.vector.memset(ques_scale_table[:].bitcast(I32), 0)
+        nc.vector.memset(img_plane1[:].bitcast(I32), 0)
 
         def load_rows(name, rows):
             raw = sb(name, [P, PACK, rows.shape[1]], F32)
@@ -73,31 +77,24 @@ def tile_attend_bilinearfuse_kernel(
             nc.sync.dma_start(out=table[:].bitcast(I32), in_=img_words[z].bitcast(I32))
             return table
 
-        nc.sync.dma_start(img_list[:], offs2)
-        nc.sync.dma_start(ques_list[:], offs)
-        gain_sb = sb("gain_sb", [P, PACK], F32)
-        nc.sync.dma_start(out=gain_sb[:], in_=gain.rearrange("(p t) o -> p (t o)", t=PACK))
         img_tables = [load_img_table(0)]
+        nc.sync.dma_start(img_list[:], offs2)
         for r in range(4):
             nc.sync.dma_start(
-                out=img_scale_table[r:P:QUAD, :, :].bitcast(I32),
+                out=img_scale_table[r:P:PASS_ROW, :].bitcast(I32),
                 in_=img_scales[:, r:16:4, :].rearrange("z q c -> q z c").bitcast(I32),
             )
         wi_raw = [load_rows("wi0_raw", wi[0:K_PASS, :])]
-        img_tables.append(load_img_table(1))
+        nc.sync.dma_start(ques_list[:], offs)
         for r in range(4):
             nc.sync.dma_start(
                 out=ques_scale_table[QUES_ROW + r : P : QUAD, :].bitcast(I32),
                 in_=ques_scales[0, r:16:4, :].bitcast(I32),
             )
         wi_raw.append(load_rows("wi1_raw", wi[K_PASS : 2 * K_PASS, :]))
-        wq_raw = load_rows("wq_raw", wq)
-        ques_table = sb("ques_table", [P, T], U32)
-        nc.sync.dma_start(
-            out=ques_table[:].bitcast(I32),
-            in_=ques_words[0].rearrange("p n t -> p (n t)").bitcast(I32),
-        )
-        wo_raw = load_rows("wo_raw", wo)
+        img_tables.append(load_img_table(1))
+        gain_sb = sb("gain_sb", [P, PACK], F32)
+        nc.sync.dma_start(out=gain_sb[:], in_=gain.rearrange("(p t) o -> p (t o)", t=PACK))
 
         def deal(name, raw, scalar_share):
             grouped = sb(f"{name}_grouped", [P, PACK, P, PACK], BF16)
@@ -122,16 +119,18 @@ def tile_attend_bilinearfuse_kernel(
             return picked
 
         img_picked = [gather("img_picked0", img_tables[0][:], img_list[:], I, U16)]
-        img_planes = [
-            gather(f"img_plane{z}", img_scale_table[:, z, :], img_list[:], I, U8) for z in range(2)
-        ]
-        img_picked.append(gather("img_picked1", img_tables[1][:], img_list[:], I, U16))
-        ques_plane = gather("ques_plane", ques_scale_table[:], ques_list[:], I, U8)
+        img_plane0 = gather("img_plane0", img_scale_table[:], img_list[:], I, U8)
+        nc.sync.dma_start(
+            out=img_plane1[0 : P - PASS_ROW, :].bitcast(I32),
+            in_=img_plane0[PASS_ROW:P, :].bitcast(I32),
+        )
+        img_planes = [img_plane0, img_plane1]
+        wq_raw = load_rows("wq_raw", wq)
 
         v_banks = [psum.tile([P, I], F32, name=f"v_bank{t}", tag=f"bank{t}") for t in range(PACK)]
-        for z in range(2):
-            share = P if z == 0 else SCALAR_SHARE
-            codes, plane = quantise(f"wi{z}", deal(f"wi{z}", wi_raw[z], share), F)
+
+        def project_images(z, scalar_share):
+            codes, plane = quantise(f"wi{z}", deal(f"wi{z}", wi_raw[z], scalar_share), F)
             for t in range(PACK):
                 cols = slice(t * P, (t + 1) * P)
                 nc.tensor.matmul_mx(
@@ -143,7 +142,30 @@ def tile_attend_bilinearfuse_kernel(
                     start=(z == 0),
                     stop=(z == 1),
                 )
-        wq_codes, wq_plane = quantise("wq", deal("wq", wq_raw, SCALAR_SHARE), F)
+
+        ques_plane = gather("ques_plane", ques_scale_table[:], ques_list[:], I, U8)
+        project_images(0, FIRST_SHARE)
+        ques_table = sb("ques_table", [P, T], U32)
+        nc.sync.dma_start(
+            out=ques_table[:].bitcast(I32),
+            in_=ques_words[0].rearrange("p n t -> p (n t)").bitcast(I32),
+        )
+        img_picked.append(gather("img_picked1", img_tables[1][:], img_list[:], I, U16))
+        wo_raw = load_rows("wo_raw", wo)
+        project_images(1, SCALAR_SHARE)
+
+        wq_codes, wq_plane = quantise("wq", deal("wq", wq_raw, 0), F)
+        tv_gain = sb("tv_gain", [P, PACK, I], F32)
+        tvs = []
+        for t in range(PACK):
+            tv = sb(f"tv{t}", [P, I], F32)
+            tvs.append(tv)
+            nc.scalar.activation(tv[:], v_banks[t][:], TANH)
+        for t in range(PACK):
+            if t < VECTOR_GAINS:
+                nc.vector.tensor_scalar(tv_gain[:, t, :], tvs[t][:], gain_sb[:, t : t + 1], None, MULT)
+            else:
+                nc.scalar.activation(tv_gain[:, t, :], tvs[t][:], COPY, scale=gain_sb[:, t : t + 1])
 
         ques_picked = []
         for g in range(I // GATHER):
@@ -151,17 +173,13 @@ def tile_attend_bilinearfuse_kernel(
             ques_picked.append(
                 gather(f"ques_picked{g}", ques_table[:], ques_list[:, columns], GATHER, U32)
             )
-
-        tv_gain = sb("tv_gain", [P, PACK, I], F32)
-        for t in range(PACK):
-            tv = sb(f"tv{t}", [P, I], F32)
-            nc.scalar.activation(tv[:], v_banks[t][:], TANH)
-            nc.vector.tensor_scalar(tv_gain[:, t, :], tv[:], gain_sb[:, t : t + 1], None, MULT)
         wo_grouped = sb("wo_grouped", [P, M, PACK], BF16)
-        nc.scalar.copy(
-            out=wo_grouped[:].rearrange("p (c e) j -> p c j e", e=2),
-            in_=wo_raw[:].rearrange("p j (c e) -> p c j e", e=2),
+        nc.vector.tensor_copy(
+            out=wo_grouped[:].rearrange("p (c e) j -> p c j e", e=4),
+            in_=wo_raw[:].rearrange("p j (c e) -> p c j e", e=4),
         )
+
+        wo_codes, wo_plane = quantise("wo", wo_grouped[:].rearrange("p m j -> p (m j)"), M)
         tz = []
         for c in range(CHUNKS):
             bank = psum.tile([P, PACK, CHUNK], F32, name=f"z_bank{c}", tag=f"bank{PACK + c}")
@@ -180,18 +198,20 @@ def tile_attend_bilinearfuse_kernel(
             tanh_z = sb(f"tz{c}", [P, PACK, CHUNK], F32)
             nc.scalar.activation(tanh_z[:], bank[:], TANH)
             tz.append(tanh_z)
-        wo_codes, wo_plane = quantise("wo", wo_grouped[:].rearrange("p m j -> p (m j)"), M)
 
         out_view = out.rearrange("(h p) i -> p h i", p=P)
-        for c in range(CHUNKS):
-            pairs = slice(c * CHUNK, (c + 1) * CHUNK)
+
+        def product(c):
             x = sb(f"x{c}", [P, CHUNK, PACK], BF16)
             nc.vector.tensor_tensor(
                 x[:].rearrange("p (c e) t -> p c t e", e=2),
                 tz[c][:].rearrange("p t (c e) -> p c t e", e=2),
-                tv_gain[:, :, pairs].rearrange("p t (c e) -> p c t e", e=2),
+                tv_gain[:, :, c * CHUNK : (c + 1) * CHUNK].rearrange("p t (c e) -> p c t e", e=2),
                 MULT,
             )
+            return x
+
+        def score(c, x):
             x_codes, x_plane = quantise(f"x{c}", x[:].rearrange("p i t -> p (i t)"), CHUNK)
             bank = psum.tile([P, M // P, CHUNK], F32, name=f"out_bank{c}", tag=f"bank{c}")
             for h in range(M // P):
@@ -207,4 +227,10 @@ def tile_attend_bilinearfuse_kernel(
                 )
             result = sb(f"result{c}", [P, M // P, CHUNK], F32)
             nc.scalar.copy(out=result[:], in_=bank[:])
-            nc.sync.dma_start(out=out_view[:, :, pairs], in_=result[:])
+            nc.sync.dma_start(out=out_view[:, :, c * CHUNK : (c + 1) * CHUNK], in_=result[:])
+
+        xs = [product(0)]
+        for c in range(CHUNKS):
+            if c + 1 < CHUNKS:
+                xs.append(product(c + 1))
+            score(c, xs[c])

@@ -14,7 +14,7 @@ U8 = mybir.dt.uint8
 FP8X4 = mybir.dt.float8_e4m3fn_x4
 FP4X4 = mybir.dt.float4_e2m1fn_x4
 TANH = mybir.ActivationFunctionType.Tanh
-COPY = mybir.ActivationFunctionType.Copy
+ADD = mybir.AluOpType.add
 MULT = mybir.AluOpType.mult
 
 P = 128
@@ -34,7 +34,6 @@ SHARED = {
     "wi0_raw": 8192, "ques_table": 8192, "wo_grouped": 8192,
     "wi0_grouped": 16384, "wi1_grouped": 16384, "wq_grouped": 16384, "ques_picked0": 16384,
     "wi1_raw": 20480, "wo_raw": 20480,
-    "tv3": 28672, "tz0": 28672,
     "ques_scale_table": 30720, "wi0_codes": 30720,
 }
 
@@ -165,7 +164,7 @@ def tile_attend_bilinearfuse_kernel(
             if t < VECTOR_GAINS:
                 nc.vector.tensor_scalar(tv_gain[:, t, :], tvs[t][:], gain_sb[:, t : t + 1], None, MULT)
             else:
-                nc.scalar.activation(tv_gain[:, t, :], tvs[t][:], COPY, scale=gain_sb[:, t : t + 1])
+                nc.gpsimd.tensor_scalar(tv_gain[:, t, :], tvs[t][:], gain_sb[:, t : t + 1], 0.0, MULT, ADD)
 
         ques_picked = []
         for g in range(I // GATHER):

@@ -14,6 +14,7 @@ U8 = mybir.dt.uint8
 FP8X4 = mybir.dt.float8_e4m3fn_x4
 FP4X4 = mybir.dt.float4_e2m1fn_x4
 TANH = mybir.ActivationFunctionType.Tanh
+COPY = mybir.ActivationFunctionType.Copy
 ADD = mybir.AluOpType.add
 MULT = mybir.AluOpType.mult
 
@@ -24,17 +25,18 @@ QUAD = 32
 CHUNK = 128
 CHUNKS = I // CHUNK
 GATHER = 256
-QUES_ROW = 8
+SPREAD_ROW = 4
+SPREAD = 8
 PASS_ROW = 16
-FIRST_SHARE = 104
-SCALAR_SHARE = 60
-VECTOR_GAINS = 2
+FIRST_SHARE = 92
+SCALAR_SHARE = 44
+WARM_PASSES = 2
 SHARED = {
     "wq_raw": 0, "img_scale_table": 0, "tv_gain": 0,
-    "wi0_raw": 8192, "ques_table": 8192, "wo_grouped": 8192,
-    "wi0_grouped": 16384, "wi1_grouped": 16384, "wq_grouped": 16384, "ques_picked0": 16384,
-    "wi1_raw": 20480, "wo_raw": 20480,
-    "ques_scale_table": 30720, "wi0_codes": 30720,
+    "wi0_codes": 8192, "ques_scale_table": 9216, "ques_table": 10240, "wo_grouped": 10240,
+    "wi0_grouped": 18432, "wi1_grouped": 18432, "wq_grouped": 18432, "ques_picked0": 18432,
+    "wi1_raw": 22528, "wo_raw": 22528,
+    "tv3": 30720, "tz0": 30720, "wo_codes": 30720,
 }
 
 
@@ -65,6 +67,8 @@ def tile_attend_bilinearfuse_kernel(
         nc.scalar.activation(warm_out[:], warm[:], TANH)
         nc.vector.memset(ques_scale_table[:].bitcast(I32), 0)
         nc.vector.memset(img_plane1[:].bitcast(I32), 0)
+        ques_plane = sb("ques_plane", [P, I], U8)
+        nc.vector.memset(ques_plane[:].bitcast(I32), 0)
 
         def load_rows(name, rows):
             raw = sb(name, [P, PACK, rows.shape[1]], F32)
@@ -84,16 +88,15 @@ def tile_attend_bilinearfuse_kernel(
                 in_=img_scales[:, r:16:4, :].rearrange("z q c -> q z c").bitcast(I32),
             )
         wi_raw = [load_rows("wi0_raw", wi[0:K_PASS, :])]
+        nc.sync.dma_start(
+            out=ques_scale_table[SPREAD_ROW:P:SPREAD, :].bitcast(I32),
+            in_=ques_scales[0].bitcast(I32),
+        )
         nc.sync.dma_start(ques_list[:], offs)
-        for r in range(4):
-            nc.sync.dma_start(
-                out=ques_scale_table[QUES_ROW + r : P : QUAD, :].bitcast(I32),
-                in_=ques_scales[0, r:16:4, :].bitcast(I32),
-            )
         wi_raw.append(load_rows("wi1_raw", wi[K_PASS : 2 * K_PASS, :]))
         img_tables.append(load_img_table(1))
         gain_sb = sb("gain_sb", [P, PACK], F32)
-        nc.sync.dma_start(out=gain_sb[:], in_=gain.rearrange("(p t) o -> p (t o)", t=PACK))
+        nc.gpsimd.dma_start(out=gain_sb[:], in_=gain.rearrange("(p t) o -> p (t o)", t=PACK))
 
         def deal(name, raw, scalar_share):
             grouped = sb(f"{name}_grouped", [P, PACK, P, PACK], BF16)
@@ -142,18 +145,35 @@ def tile_attend_bilinearfuse_kernel(
                     stop=(z == 1),
                 )
 
-        ques_plane = gather("ques_plane", ques_scale_table[:], ques_list[:], I, U8)
-        project_images(0, FIRST_SHARE)
+        ques_spread = gather("ques_spread", ques_scale_table[:], ques_list[:], I, U8)
+        for r in range(4):
+            nc.sync.dma_start(
+                out=ques_plane[r:P:QUAD, :].bitcast(I32),
+                in_=ques_spread[SPREAD_ROW + SPREAD * r : P : QUAD, :].bitcast(I32),
+            )
         ques_table = sb("ques_table", [P, T], U32)
         nc.sync.dma_start(
             out=ques_table[:].bitcast(I32),
             in_=ques_words[0].rearrange("p n t -> p (n t)").bitcast(I32),
         )
+        project_images(0, FIRST_SHARE)
         img_picked.append(gather("img_picked1", img_tables[1][:], img_list[:], I, U16))
         wo_raw = load_rows("wo_raw", wo)
         project_images(1, SCALAR_SHARE)
 
         wq_codes, wq_plane = quantise("wq", deal("wq", wq_raw, 0), F)
+        warm_bank = psum.tile([P, I], F32, name="warm_bank", tag=f"bank{2 * PACK - 1}")
+        for t in range(WARM_PASSES):
+            cols = slice(t * P, (t + 1) * P)
+            nc.tensor.matmul_mx(
+                out=warm_bank[:],
+                lhsT=wq_codes[:, cols].bitcast(FP8X4),
+                lhsT_scale=wq_plane[:, cols],
+                rhs=img_picked[1][:].bitcast(FP4X4),
+                rhs_scale=img_planes[1][:],
+                start=True,
+                stop=True,
+            )
         tv_gain = sb("tv_gain", [P, PACK, I], F32)
         tvs = []
         for t in range(PACK):
@@ -161,10 +181,13 @@ def tile_attend_bilinearfuse_kernel(
             tvs.append(tv)
             nc.scalar.activation(tv[:], v_banks[t][:], TANH)
         for t in range(PACK):
-            if t < VECTOR_GAINS:
-                nc.vector.tensor_scalar(tv_gain[:, t, :], tvs[t][:], gain_sb[:, t : t + 1], None, MULT)
+            factor = gain_sb[:, t : t + 1]
+            if t == 0:
+                nc.vector.tensor_scalar(tv_gain[:, t, :], tvs[t][:], factor, None, MULT)
+            elif t + 1 < PACK:
+                nc.gpsimd.tensor_scalar(tv_gain[:, t, :], tvs[t][:], factor, 0.0, MULT, ADD)
             else:
-                nc.gpsimd.tensor_scalar(tv_gain[:, t, :], tvs[t][:], gain_sb[:, t : t + 1], 0.0, MULT, ADD)
+                nc.scalar.activation(tv_gain[:, t, :], tvs[t][:], COPY, scale=factor)
 
         ques_picked = []
         for g in range(I // GATHER):
@@ -178,7 +201,6 @@ def tile_attend_bilinearfuse_kernel(
             in_=wo_raw[:].rearrange("p j (c e) -> p c j e", e=4),
         )
 
-        wo_codes, wo_plane = quantise("wo", wo_grouped[:].rearrange("p m j -> p (m j)"), M)
         tz = []
         for c in range(CHUNKS):
             bank = psum.tile([P, PACK, CHUNK], F32, name=f"z_bank{c}", tag=f"bank{PACK + c}")
@@ -190,7 +212,7 @@ def tile_attend_bilinearfuse_kernel(
                     lhsT=wq_codes[:, cols].bitcast(FP8X4),
                     lhsT_scale=wq_plane[:, cols],
                     rhs=ques_picked[g][:, first : first + CHUNK].bitcast(FP8X4),
-                    rhs_scale=ques_plane[QUES_ROW:P, c * CHUNK : (c + 1) * CHUNK],
+                    rhs_scale=ques_plane[:, c * CHUNK : (c + 1) * CHUNK],
                     start=True,
                     stop=True,
                 )
@@ -210,25 +232,39 @@ def tile_attend_bilinearfuse_kernel(
             )
             return x
 
+        def answer(bank, h, x_codes, x_plane):
+            cols = slice(h * P, (h + 1) * P)
+            nc.tensor.matmul_mx(
+                out=bank,
+                lhsT=wo_codes[:, cols].bitcast(FP8X4),
+                lhsT_scale=wo_plane[:, cols],
+                rhs=x_codes[:].bitcast(FP8X4),
+                rhs_scale=x_plane[:],
+                start=True,
+                stop=True,
+            )
+
         def score(c, x):
             x_codes, x_plane = quantise(f"x{c}", x[:].rearrange("p i t -> p (i t)"), CHUNK)
-            bank = psum.tile([P, M // P, CHUNK], F32, name=f"out_bank{c}", tag=f"bank{c}")
-            for h in range(M // P):
-                cols = slice(h * P, (h + 1) * P)
-                nc.tensor.matmul_mx(
-                    out=bank[:, h, :],
-                    lhsT=wo_codes[:, cols].bitcast(FP8X4),
-                    lhsT_scale=wo_plane[:, cols],
-                    rhs=x_codes[:].bitcast(FP8X4),
-                    rhs_scale=x_plane[:],
-                    start=True,
-                    stop=True,
-                )
-            result = sb(f"result{c}", [P, M // P, CHUNK], F32)
-            nc.scalar.copy(out=result[:], in_=bank[:])
-            nc.sync.dma_start(out=out_view[:, :, c * CHUNK : (c + 1) * CHUNK], in_=result[:])
+            pairs = slice(c * CHUNK, (c + 1) * CHUNK)
+            if c + 1 < CHUNKS:
+                bank = psum.tile([P, M // P, CHUNK], F32, name=f"out_bank{c}", tag=f"bank{c}")
+                for h in range(M // P):
+                    answer(bank[:, h, :], h, x_codes, x_plane)
+                result = sb(f"result{c}", [P, M // P, CHUNK], F32)
+                nc.scalar.copy(out=result[:], in_=bank[:])
+                nc.sync.dma_start(out=out_view[:, :, pairs], in_=result[:])
+            else:
+                ways = [(nc.vector.tensor_copy, nc.sync), (nc.scalar.copy, nc.sync)]
+                for h, (copy_out, queue) in enumerate(ways):
+                    bank = psum.tile([P, CHUNK], F32, name=f"last_bank{h}", tag=f"bank{c + h}")
+                    answer(bank[:], h, x_codes, x_plane)
+                    result = sb(f"last_result{h}", [P, CHUNK], F32)
+                    copy_out(out=result[:], in_=bank[:])
+                    queue.dma_start(out=out_view[:, h, pairs], in_=result[:])
 
         xs = [product(0)]
+        wo_codes, wo_plane = quantise("wo", wo_grouped[:].rearrange("p m j -> p (m j)"), M)
         for c in range(CHUNKS):
             if c + 1 < CHUNKS:
                 xs.append(product(c + 1))

@@ -60,11 +60,7 @@ def tile_attend_bilinearfuse_kernel(
         img_scale_table = sb("img_scale_table", [P, U], U8)
         ques_scale_table = sb("ques_scale_table", [P, T], U8)
         img_plane1 = sb("img_plane1", [P, I], U8)
-        warm = sb("warm", [P, 8], F32)
-        warm_out = sb("warm_out", [P, 8], F32)
         nc.vector.memset(img_scale_table[:].bitcast(I32), 0)
-        nc.vector.memset(warm[:], 0.0)
-        nc.scalar.activation(warm_out[:], warm[:], TANH)
         nc.vector.memset(ques_scale_table[:].bitcast(I32), 0)
         nc.vector.memset(img_plane1[:].bitcast(I32), 0)
         ques_plane = sb("ques_plane", [P, I], U8)

@@ -32,11 +32,11 @@ FIRST_SHARE = 92
 SCALAR_SHARE = 44
 WARM_PASSES = 2
 SHARED = {
-    "wq_raw": 0, "img_scale_table": 0, "tv_gain": 0,
+    "wq_raw": 0, "img_table0": 0, "tv_gain": 0,
     "wi0_codes": 8192, "ques_scale_table": 9216, "ques_table": 10240, "wo_grouped": 10240,
     "wi0_grouped": 18432, "wi1_grouped": 18432, "wq_grouped": 18432, "ques_picked0": 18432,
-    "wi1_raw": 22528, "wo_raw": 22528,
-    "tv3": 30720, "tz0": 30720, "wo_codes": 30720,
+    "wi1_raw": 22528, "wo_raw": 22528, "img_scale_table": 29696, "img_table1": 30720,
+    "tv3": 34816, "tz0": 34816, "wo_codes": 34816,
 }
 
 
@@ -59,12 +59,13 @@ def tile_attend_bilinearfuse_kernel(
 
         img_scale_table = sb("img_scale_table", [P, U], U8)
         ques_scale_table = sb("ques_scale_table", [P, T], U8)
-        img_plane1 = sb("img_plane1", [P, I], U8)
-        nc.vector.memset(img_scale_table[:].bitcast(I32), 0)
+        nc.vector.memset(img_scale_table[QUAD : 2 * QUAD, :].bitcast(I32), 0)
+        nc.vector.memset(img_scale_table[2 * QUAD : P, :].bitcast(I32), 0)
         nc.vector.memset(ques_scale_table[:].bitcast(I32), 0)
-        nc.vector.memset(img_plane1[:].bitcast(I32), 0)
+        img_planes = [sb(f"img_plane{z}", [P, I], U8) for z in range(2)]
         ques_plane = sb("ques_plane", [P, I], U8)
-        nc.vector.memset(ques_plane[:].bitcast(I32), 0)
+        for plane in img_planes + [ques_plane]:
+            nc.vector.memset(plane[:].bitcast(I32), 0)
 
         def load_rows(name, rows):
             raw = sb(name, [P, PACK, rows.shape[1]], F32)
@@ -76,21 +77,18 @@ def tile_attend_bilinearfuse_kernel(
             nc.sync.dma_start(out=table[:].bitcast(I32), in_=img_words[z].bitcast(I32))
             return table
 
-        img_tables = [load_img_table(0)]
         nc.sync.dma_start(img_list[:], offs2)
-        for r in range(4):
-            nc.sync.dma_start(
-                out=img_scale_table[r:P:PASS_ROW, :].bitcast(I32),
-                in_=img_scales[:, r:16:4, :].rearrange("z q c -> q z c").bitcast(I32),
-            )
+        nc.sync.dma_start(
+            out=img_scale_table[0:QUAD, :].bitcast(I32),
+            in_=img_scales.rearrange("z q c -> (z q) c").bitcast(I32),
+        )
+        img_tables = [load_img_table(0)]
         wi_raw = [load_rows("wi0_raw", wi[0:K_PASS, :])]
         nc.sync.dma_start(
             out=ques_scale_table[SPREAD_ROW:P:SPREAD, :].bitcast(I32),
             in_=ques_scales[0].bitcast(I32),
         )
         nc.sync.dma_start(ques_list[:], offs)
-        wi_raw.append(load_rows("wi1_raw", wi[K_PASS : 2 * K_PASS, :]))
-        img_tables.append(load_img_table(1))
         gain_sb = sb("gain_sb", [P, PACK], F32)
         nc.gpsimd.dma_start(out=gain_sb[:], in_=gain.rearrange("(p t) o -> p (t o)", t=PACK))
 
@@ -116,13 +114,21 @@ def tile_attend_bilinearfuse_kernel(
             nc.vector.tensor_copy(picked[:], window.indirect(offsets))
             return picked
 
+        img_rows = gather("img_rows", img_scale_table[:], img_list[:], I, U8)
         img_picked = [gather("img_picked0", img_tables[0][:], img_list[:], I, U16)]
-        img_plane0 = gather("img_plane0", img_scale_table[:], img_list[:], I, U8)
-        nc.sync.dma_start(
-            out=img_plane1[0 : P - PASS_ROW, :].bitcast(I32),
-            in_=img_plane0[PASS_ROW:P, :].bitcast(I32),
-        )
-        img_planes = [img_plane0, img_plane1]
+
+        def lay_img_plane(z):
+            for q in range(4):
+                first = PASS_ROW * z + 4 * q
+                nc.sync.dma_start(
+                    out=img_planes[z][QUAD * q : QUAD * q + 4, :].bitcast(I32),
+                    in_=img_rows[first : first + 4, :].bitcast(I32),
+                )
+
+        lay_img_plane(0)
+        wi_raw.append(load_rows("wi1_raw", wi[K_PASS : 2 * K_PASS, :]))
+        lay_img_plane(1)
+        img_tables.append(load_img_table(1))
         wq_raw = load_rows("wq_raw", wq)
 
         v_banks = [psum.tile([P, I], F32, name=f"v_bank{t}", tag=f"bank{t}") for t in range(PACK)]

@@ -28,15 +28,15 @@ GATHER = 256
 SPREAD_ROW = 4
 SPREAD = 8
 PASS_ROW = 16
-FIRST_SHARE = 92
-SCALAR_SHARE = 44
+PAIR = 2
 WARM_PASSES = 2
 SHARED = {
-    "wq_raw": 0, "img_table0": 0, "tv_gain": 0,
-    "wi0_codes": 8192, "ques_scale_table": 9216, "ques_table": 10240, "wo_grouped": 10240,
-    "wi0_grouped": 18432, "wi1_grouped": 18432, "wq_grouped": 18432, "ques_picked0": 18432,
-    "wi1_raw": 22528, "wo_raw": 22528, "img_scale_table": 29696, "img_table1": 30720,
-    "tv3": 34816, "tz0": 34816, "wo_codes": 34816,
+    "wq_raw": 256, "ques_scale_table": 8192, "wi0_codes0": 8448, "ques_table": 9472,
+    "wo_grouped0": 10240, "wo_grouped1": 11264,
+    "wq_grouped1": 18432, "tv_gain": 18432,
+    "wi1_raw": 26624, "wo_raw": 26624, "img_scale_table": 33792, "img_table1": 34816, "wi1_codes1": 34816,
+    "tv3": 38912, "tz0": 38912, "tz1": 39936,
+    "wq_grouped0": 40960, "ques_picked0": 40960,
 }
 
 
@@ -92,20 +92,19 @@ def tile_attend_bilinearfuse_kernel(
         gain_sb = sb("gain_sb", [P, PACK], F32)
         nc.gpsimd.dma_start(out=gain_sb[:], in_=gain.rearrange("(p t) o -> p (t o)", t=PACK))
 
-        def deal(name, raw, scalar_share):
-            grouped = sb(f"{name}_grouped", [P, PACK, P, PACK], BF16)
-            parts = [(nc.scalar.copy, 0, scalar_share), (nc.vector.tensor_copy, scalar_share, P)]
-            for copy_part, lo, hi in parts:
-                if lo < hi:
-                    copy_part(
-                        out=grouped[:, :, lo:hi, :].rearrange("p t m j -> p m j t"),
-                        in_=raw[:, :, lo * PACK : hi * PACK].rearrange("p j (m t) -> p m j t", t=PACK),
-                    )
-            return grouped[:].rearrange("p t m j -> p (t m j)")
+        def deal(name, raw, shares):
+            halves = [sb(f"{name}_grouped{u}", [P, PAIR, P, PACK], BF16) for u in range(PACK // PAIR)]
+            for copy_part, u, lo, hi in shares:
+                copy_part(
+                    out=halves[u][:, :, lo:hi, :].rearrange("p t m j -> p m j t"),
+                    in_=raw[:]
+                    .rearrange("p j (m t) -> p m j t", t=PACK)[:, lo:hi, :, u * PAIR : (u + 1) * PAIR],
+                )
+            return [half[:].rearrange("p t m j -> p (t m j)") for half in halves]
 
         def quantise(name, values, width):
-            codes = sb(f"{name}_codes", [P, width], U32)
-            plane = sb(f"{name}_plane", [P, width], U8)
+            codes = sb(name.replace("_", "_codes"), [P, width], U32)
+            plane = sb(name.replace("_", "_plane"), [P, width], U8)
             nc.vector.quantize_mx(out=codes[:].bitcast(FP8X4), scales=plane[:], in_=values)
             return codes, plane
 
@@ -129,25 +128,31 @@ def tile_attend_bilinearfuse_kernel(
         wi_raw.append(load_rows("wi1_raw", wi[K_PASS : 2 * K_PASS, :]))
         lay_img_plane(1)
         img_tables.append(load_img_table(1))
-        wq_raw = load_rows("wq_raw", wq)
 
         v_banks = [psum.tile([P, I], F32, name=f"v_bank{t}", tag=f"bank{t}") for t in range(PACK)]
 
-        def project_images(z, scalar_share):
-            codes, plane = quantise(f"wi{z}", deal(f"wi{z}", wi_raw[z], scalar_share), F)
-            for t in range(PACK):
-                cols = slice(t * P, (t + 1) * P)
+        def feature_tile(halves, t):
+            codes, plane = halves[t // PAIR]
+            cols = slice(t % PAIR * P, (t % PAIR + 1) * P)
+            return codes[:, cols].bitcast(FP8X4), plane[:, cols]
+
+        def image_passes(z, u, half):
+            for t in range(u * PAIR, (u + 1) * PAIR):
+                codes, plane = feature_tile({u: half}, t)
                 nc.tensor.matmul_mx(
                     out=v_banks[t][:],
-                    lhsT=codes[:, cols].bitcast(FP8X4),
-                    lhsT_scale=plane[:, cols],
+                    lhsT=codes,
+                    lhsT_scale=plane,
                     rhs=img_picked[z][:].bitcast(FP4X4),
                     rhs_scale=img_planes[z][:],
                     start=(z == 0),
                     stop=(z == 1),
                 )
 
+        on_scalar, on_vector = nc.scalar.copy, nc.vector.tensor_copy
+
         ques_spread = gather("ques_spread", ques_scale_table[:], ques_list[:], I, U8)
+        wq_raw = load_rows("wq_raw", wq)
         for r in range(4):
             nc.sync.dma_start(
                 out=ques_plane[r:P:QUAD, :].bitcast(I32),
@@ -158,19 +163,25 @@ def tile_attend_bilinearfuse_kernel(
             out=ques_table[:].bitcast(I32),
             in_=ques_words[0].rearrange("p n t -> p (n t)").bitcast(I32),
         )
-        project_images(0, FIRST_SHARE)
+        dealt = deal("wi0", wi_raw[0], [(on_scalar, 0, 0, P), (on_scalar, 1, 0, 40), (on_vector, 1, 40, P)])
+        for u in range(PACK // PAIR):
+            image_passes(0, u, quantise(f"wi0_{u}", dealt[u], PAIR * P))
+        dealt = deal("wi1", wi_raw[1], [(on_vector, 0, 0, P), (on_scalar, 1, 0, P)])
+        wi1_first = quantise("wi1_0", dealt[0], PAIR * P)
         img_picked.append(gather("img_picked1", img_tables[1][:], img_list[:], I, U16))
         wo_raw = load_rows("wo_raw", wo)
-        project_images(1, SCALAR_SHARE)
+        image_passes(1, 0, wi1_first)
+        image_passes(1, 1, quantise("wi1_1", dealt[1], PAIR * P))
 
-        wq_codes, wq_plane = quantise("wq", deal("wq", wq_raw, 0), F)
+        dealt = deal("wq", wq_raw, [(on_vector, 0, 0, P), (on_vector, 1, 0, P)])
+        wq_halves = [quantise(f"wq_{u}", dealt[u], PAIR * P) for u in range(PACK // PAIR)]
         warm_bank = psum.tile([P, I], F32, name="warm_bank", tag=f"bank{2 * PACK - 1}")
         for t in range(WARM_PASSES):
-            cols = slice(t * P, (t + 1) * P)
+            codes, plane = feature_tile(wq_halves, t)
             nc.tensor.matmul_mx(
                 out=warm_bank[:],
-                lhsT=wq_codes[:, cols].bitcast(FP8X4),
-                lhsT_scale=wq_plane[:, cols],
+                lhsT=codes,
+                lhsT_scale=plane,
                 rhs=img_picked[1][:].bitcast(FP4X4),
                 rhs_scale=img_planes[1][:],
                 start=True,
@@ -184,9 +195,7 @@ def tile_attend_bilinearfuse_kernel(
             nc.scalar.activation(tv[:], v_banks[t][:], TANH)
         for t in range(PACK):
             factor = gain_sb[:, t : t + 1]
-            if t == 0:
-                nc.vector.tensor_scalar(tv_gain[:, t, :], tvs[t][:], factor, None, MULT)
-            elif t + 1 < PACK:
+            if t < PAIR:
                 nc.gpsimd.tensor_scalar(tv_gain[:, t, :], tvs[t][:], factor, 0.0, MULT, ADD)
             else:
                 nc.scalar.activation(tv_gain[:, t, :], tvs[t][:], COPY, scale=factor)
@@ -197,49 +206,59 @@ def tile_attend_bilinearfuse_kernel(
             ques_picked.append(
                 gather(f"ques_picked{g}", ques_table[:], ques_list[:, columns], GATHER, U32)
             )
-        wo_grouped = sb("wo_grouped", [P, M, PACK], BF16)
-        nc.vector.tensor_copy(
-            out=wo_grouped[:].rearrange("p (c e) j -> p c j e", e=4),
-            in_=wo_raw[:].rearrange("p j (c e) -> p c j e", e=4),
-        )
+        wo_halves = []
+        for h in range(M // P):
+            grouped = sb(f"wo_grouped{h}", [P, P, PACK], BF16)
+            nc.vector.tensor_copy(
+                out=grouped[:].rearrange("p (c e) j -> p c j e", e=4),
+                in_=wo_raw[:, :, h * P : (h + 1) * P].rearrange("p j (c e) -> p c j e", e=4),
+            )
+            wo_halves.append(grouped)
+        wo_halves = [
+            quantise(f"wo_{h}", grouped[:].rearrange("p m j -> p (m j)"), P)
+            for h, grouped in enumerate(wo_halves)
+        ]
 
+        half = CHUNK // 2
+        pieces = [(0, half), (half, CHUNK)] + [(c * CHUNK, (c + 1) * CHUNK) for c in range(1, CHUNKS)]
+        z_tags = [PACK, 0] + [PACK + c for c in range(1, CHUNKS)]
         tz = []
-        for c in range(CHUNKS):
-            bank = psum.tile([P, PACK, CHUNK], F32, name=f"z_bank{c}", tag=f"bank{PACK + c}")
-            g, first = divmod(c * CHUNK, GATHER)
+        for n, (lo, hi) in enumerate(pieces):
+            bank = psum.tile([P, PACK, hi - lo], F32, name=f"z_bank{n}", tag=f"bank{z_tags[n]}")
+            g, first = divmod(lo, GATHER)
             for t in range(PACK):
-                cols = slice(t * P, (t + 1) * P)
+                codes, plane = feature_tile(wq_halves, t)
                 nc.tensor.matmul_mx(
                     out=bank[:, t, :],
-                    lhsT=wq_codes[:, cols].bitcast(FP8X4),
-                    lhsT_scale=wq_plane[:, cols],
-                    rhs=ques_picked[g][:, first : first + CHUNK].bitcast(FP8X4),
-                    rhs_scale=ques_plane[:, c * CHUNK : (c + 1) * CHUNK],
+                    lhsT=codes,
+                    lhsT_scale=plane,
+                    rhs=ques_picked[g][:, first : first + hi - lo].bitcast(FP8X4),
+                    rhs_scale=ques_plane[:, lo:hi],
                     start=True,
                     stop=True,
                 )
-            tanh_z = sb(f"tz{c}", [P, PACK, CHUNK], F32)
+            tanh_z = sb(f"tz{n}", [P, PACK, hi - lo], F32)
             nc.scalar.activation(tanh_z[:], bank[:], TANH)
             tz.append(tanh_z)
 
         out_view = out.rearrange("(h p) i -> p h i", p=P)
 
-        def product(c):
-            x = sb(f"x{c}", [P, CHUNK, PACK], BF16)
+        def product(lo, hi):
+            n = max(k for k, piece in enumerate(pieces) if piece[0] <= lo)
+            c, first = divmod(lo, CHUNK)
             nc.vector.tensor_tensor(
-                x[:].rearrange("p (c e) t -> p c t e", e=2),
-                tz[c][:].rearrange("p t (c e) -> p c t e", e=2),
-                tv_gain[:, :, c * CHUNK : (c + 1) * CHUNK].rearrange("p t (c e) -> p c t e", e=2),
+                xs[c][:, first : first + hi - lo, :].rearrange("p (c e) t -> p c t e", e=2),
+                tz[n][:, :, lo - pieces[n][0] : hi - pieces[n][0]].rearrange("p t (c e) -> p c t e", e=2),
+                tv_gain[:, :, lo:hi].rearrange("p t (c e) -> p c t e", e=2),
                 MULT,
             )
-            return x
 
         def answer(bank, h, x_codes, x_plane):
-            cols = slice(h * P, (h + 1) * P)
+            codes, plane = wo_halves[h]
             nc.tensor.matmul_mx(
                 out=bank,
-                lhsT=wo_codes[:, cols].bitcast(FP8X4),
-                lhsT_scale=wo_plane[:, cols],
+                lhsT=codes[:].bitcast(FP8X4),
+                lhsT_scale=plane[:],
                 rhs=x_codes[:].bitcast(FP8X4),
                 rhs_scale=x_plane[:],
                 start=True,
@@ -247,10 +266,10 @@ def tile_attend_bilinearfuse_kernel(
             )
 
         def score(c, x):
-            x_codes, x_plane = quantise(f"x{c}", x[:].rearrange("p i t -> p (i t)"), CHUNK)
+            x_codes, x_plane = quantise(f"x_{c}", x[:].rearrange("p i t -> p (i t)"), CHUNK)
             pairs = slice(c * CHUNK, (c + 1) * CHUNK)
             if c + 1 < CHUNKS:
-                bank = psum.tile([P, M // P, CHUNK], F32, name=f"out_bank{c}", tag=f"bank{c}")
+                bank = psum.tile([P, M // P, CHUNK], F32, name=f"out_bank{c}", tag=f"bank{c + 1}")
                 for h in range(M // P):
                     answer(bank[:, h, :], h, x_codes, x_plane)
                 result = sb(f"result{c}", [P, M // P, CHUNK], F32)
@@ -259,15 +278,20 @@ def tile_attend_bilinearfuse_kernel(
             else:
                 ways = [(nc.vector.tensor_copy, nc.sync), (nc.scalar.copy, nc.sync)]
                 for h, (copy_out, queue) in enumerate(ways):
-                    bank = psum.tile([P, CHUNK], F32, name=f"last_bank{h}", tag=f"bank{c + h}")
+                    bank = psum.tile([P, CHUNK], F32, name=f"last_bank{h}", tag=f"bank{z_tags[h]}")
                     answer(bank[:], h, x_codes, x_plane)
                     result = sb(f"last_result{h}", [P, CHUNK], F32)
                     copy_out(out=result[:], in_=bank[:])
                     queue.dma_start(out=out_view[:, h, pairs], in_=result[:])
 
-        xs = [product(0)]
-        wo_codes, wo_plane = quantise("wo", wo_grouped[:].rearrange("p m j -> p (m j)"), M)
-        for c in range(CHUNKS):
-            if c + 1 < CHUNKS:
-                xs.append(product(c + 1))
-            score(c, xs[c])
+        xs = [sb(f"x{c}", [P, CHUNK, PACK], BF16) for c in range(CHUNKS)]
+        last = CHUNKS - 1
+        product(0, half)
+        product(half, CHUNK)
+        for c in range(1, last):
+            product(c * CHUNK, (c + 1) * CHUNK)
+            score(c - 1, xs[c - 1])
+        product(last * CHUNK, I - half)
+        score(last - 1, xs[last - 1])
+        product(I - half, I)
+        score(last, xs[last])

@@ -32,10 +32,10 @@ PAIR = 2
 WARM_PASSES = 2
 SHARED = {
     "wq_raw": 256, "ques_scale_table": 8192, "wi0_codes0": 8448, "ques_table": 9472,
-    "wo_grouped0": 10240, "wo_grouped1": 11264,
+    "wo_grouped0": 10240, "x_all": 7168, "wo_grouped1": 11264,
     "wq_grouped1": 18432, "tv_gain": 18432,
     "wi1_raw": 26624, "wo_raw": 26624, "img_scale_table": 33792, "img_table1": 34816, "wi1_codes1": 34816,
-    "tv3": 38912, "tz0": 38912, "tz1": 39936,
+    "tv3": 43008, "tanh_z": 43008,
     "wq_grouped0": 40960, "ques_picked0": 40960,
 }
 
@@ -153,16 +153,16 @@ def tile_attend_bilinearfuse_kernel(
 
         ques_spread = gather("ques_spread", ques_scale_table[:], ques_list[:], I, U8)
         wq_raw = load_rows("wq_raw", wq)
-        for r in range(4):
-            nc.sync.dma_start(
-                out=ques_plane[r:P:QUAD, :].bitcast(I32),
-                in_=ques_spread[SPREAD_ROW + SPREAD * r : P : QUAD, :].bitcast(I32),
-            )
         ques_table = sb("ques_table", [P, T], U32)
         nc.sync.dma_start(
             out=ques_table[:].bitcast(I32),
             in_=ques_words[0].rearrange("p n t -> p (n t)").bitcast(I32),
         )
+        for r in range(4):
+            nc.sync.dma_start(
+                out=ques_plane[r:P:QUAD, :].bitcast(I32),
+                in_=ques_spread[SPREAD_ROW + SPREAD * r : P : QUAD, :].bitcast(I32),
+            )
         dealt = deal("wi0", wi_raw[0], [(on_scalar, 0, 0, P), (on_scalar, 1, 0, 40), (on_vector, 1, 40, P)])
         for u in range(PACK // PAIR):
             image_passes(0, u, quantise(f"wi0_{u}", dealt[u], PAIR * P))
@@ -223,6 +223,7 @@ def tile_attend_bilinearfuse_kernel(
         pieces = [(0, half), (half, CHUNK)] + [(c * CHUNK, (c + 1) * CHUNK) for c in range(1, CHUNKS)]
         z_tags = [PACK, 0] + [PACK + c for c in range(1, CHUNKS)]
         tz = []
+        tanh_z = sb("tanh_z", [P, PACK * I], F32)
         for n, (lo, hi) in enumerate(pieces):
             bank = psum.tile([P, PACK, hi - lo], F32, name=f"z_bank{n}", tag=f"bank{z_tags[n]}")
             g, first = divmod(lo, GATHER)
@@ -237,9 +238,9 @@ def tile_attend_bilinearfuse_kernel(
                     start=True,
                     stop=True,
                 )
-            tanh_z = sb(f"tz{n}", [P, PACK, hi - lo], F32)
-            nc.scalar.activation(tanh_z[:], bank[:], TANH)
-            tz.append(tanh_z)
+            piece = tanh_z[:, PACK * lo : PACK * hi]
+            nc.scalar.activation(piece, bank[:].rearrange("p t i -> p (t i)"), TANH)
+            tz.append(piece.rearrange("p (t i) -> p t i", t=PACK))
 
         out_view = out.rearrange("(h p) i -> p h i", p=P)
 
@@ -266,7 +267,7 @@ def tile_attend_bilinearfuse_kernel(
             )
 
         def score(c, x):
-            x_codes, x_plane = quantise(f"x_{c}", x[:].rearrange("p i t -> p (i t)"), CHUNK)
+            x_codes, x_plane = quantise(f"x_{c}", x.rearrange("p i t -> p (i t)"), CHUNK)
             pairs = slice(c * CHUNK, (c + 1) * CHUNK)
             if c + 1 < CHUNKS:
                 bank = psum.tile([P, M // P, CHUNK], F32, name=f"out_bank{c}", tag=f"bank{c + 1}")
@@ -284,7 +285,11 @@ def tile_attend_bilinearfuse_kernel(
                     copy_out(out=result[:], in_=bank[:])
                     queue.dma_start(out=out_view[:, h, pairs], in_=result[:])
 
-        xs = [sb(f"x{c}", [P, CHUNK, PACK], BF16) for c in range(CHUNKS)]
+        x_all = sb("x_all", [P, I * PACK], BF16)
+        xs = [
+            x_all[:, c * CHUNK * PACK : (c + 1) * CHUNK * PACK].rearrange("p (i t) -> p i t", t=PACK)
+            for c in range(CHUNKS)
+        ]
         last = CHUNKS - 1
         product(0, half)
         product(half, CHUNK)

@@ -33,10 +33,10 @@ WARM_PASSES = 2
 SHARED = {
     "wq_raw": 256, "ques_scale_table": 8192, "wi0_codes0": 8448, "ques_table": 9472,
     "wo_grouped0": 10240, "x_all": 7168, "wo_grouped1": 11264,
-    "wq_grouped1": 18432, "tv_gain": 18432,
+    "wq_grouped0": 18432, "tv_gain": 18432,
     "wi1_raw": 26624, "wo_raw": 26624, "img_scale_table": 33792, "img_table1": 34816, "wi1_codes1": 34816,
     "tv3": 43008, "tanh_z": 43008,
-    "wq_grouped0": 40960, "ques_picked0": 40960,
+    "tv0": 40960, "ques_picked0": 40960,
 }
 
 
@@ -196,7 +196,7 @@ def tile_attend_bilinearfuse_kernel(
         for t in range(PACK):
             factor = gain_sb[:, t : t + 1]
             if t < PAIR:
-                nc.gpsimd.tensor_scalar(tv_gain[:, t, :], tvs[t][:], factor, 0.0, MULT, ADD)
+                nc.vector.tensor_scalar(tv_gain[:, t, :], tvs[t][:], factor, None, MULT)
             else:
                 nc.scalar.activation(tv_gain[:, t, :], tvs[t][:], COPY, scale=factor)
 

@@ -33,10 +33,10 @@ WARM_PASSES = 2
 SHARED = {
     "wq_raw": 256, "ques_scale_table": 8192, "wi0_codes0": 8448, "ques_table": 9472,
     "wo_grouped0": 10240, "x_all": 7168, "wo_grouped1": 11264,
-    "wq_grouped0": 18432, "tv_gain": 18432,
+    "wq_grouped0": 18432, "ques_picked0": 18432,
     "wi1_raw": 26624, "wo_raw": 26624, "img_scale_table": 33792, "img_table1": 34816, "wi1_codes1": 34816,
-    "tv3": 43008, "tanh_z": 43008,
-    "tv0": 40960, "ques_picked0": 40960,
+    "tv1": 43008, "tanh_z": 43008,
+
 }
 
 
@@ -129,7 +129,9 @@ def tile_attend_bilinearfuse_kernel(
         lay_img_plane(1)
         img_tables.append(load_img_table(1))
 
-        v_banks = [psum.tile([P, I], F32, name=f"v_bank{t}", tag=f"bank{t}") for t in range(PACK)]
+        v_banks = [
+            psum.tile([P, PAIR, GATHER], F32, name=f"v_bank{b}", tag=f"bank{b}") for b in range(PACK)
+        ]
 
         def feature_tile(halves, t):
             codes, plane = halves[t // PAIR]
@@ -137,17 +139,20 @@ def tile_attend_bilinearfuse_kernel(
             return codes[:, cols].bitcast(FP8X4), plane[:, cols]
 
         def image_passes(z, u, half):
-            for t in range(u * PAIR, (u + 1) * PAIR):
-                codes, plane = feature_tile({u: half}, t)
-                nc.tensor.matmul_mx(
-                    out=v_banks[t][:],
-                    lhsT=codes,
-                    lhsT_scale=plane,
-                    rhs=img_picked[z][:].bitcast(FP4X4),
-                    rhs_scale=img_planes[z][:],
-                    start=(z == 0),
-                    stop=(z == 1),
-                )
+            for g in range(I // GATHER):
+                spots = [(t, c) for t in range(PAIR) for c in range(GATHER // CHUNK)]
+                for t, c in spots:
+                    codes, plane = feature_tile([half], t)
+                    pairs = slice(g * GATHER + c * CHUNK, g * GATHER + (c + 1) * CHUNK)
+                    nc.tensor.matmul_mx(
+                        out=v_banks[PAIR * u + g][:, t, c * CHUNK : (c + 1) * CHUNK],
+                        lhsT=codes,
+                        lhsT_scale=plane,
+                        rhs=img_picked[z][:, pairs].bitcast(FP4X4),
+                        rhs_scale=img_planes[z][:, pairs],
+                        start=(z == 0 and (t, c) == spots[0]),
+                        stop=(z == 1 and (t, c) == spots[-1]),
+                    )
 
         on_scalar, on_vector = nc.scalar.copy, nc.vector.tensor_copy
 
@@ -168,7 +173,12 @@ def tile_attend_bilinearfuse_kernel(
             image_passes(0, u, quantise(f"wi0_{u}", dealt[u], PAIR * P))
         dealt = deal("wi1", wi_raw[1], [(on_vector, 0, 0, P), (on_scalar, 1, 0, P)])
         wi1_first = quantise("wi1_0", dealt[0], PAIR * P)
-        img_picked.append(gather("img_picked1", img_tables[1][:], img_list[:], I, U16))
+        img_picked.append(sb("img_picked1", [P, I], U16))
+        for g in range(I // GATHER):
+            nc.vector.tensor_copy(
+                img_picked[1][:, g * GATHER : (g + 1) * GATHER],
+                img_tables[1][:].indirect(img_list[:, g * GATHER // 16 : (g + 1) * GATHER // 16]),
+            )
         wo_raw = load_rows("wo_raw", wo)
         image_passes(1, 0, wi1_first)
         image_passes(1, 1, quantise("wi1_1", dealt[1], PAIR * P))
@@ -188,17 +198,18 @@ def tile_attend_bilinearfuse_kernel(
                 stop=True,
             )
         tv_gain = sb("tv_gain", [P, PACK, I], F32)
-        tvs = []
+        tvs = [sb(f"tv{u}", [P, PAIR, I], F32) for u in range(PACK // PAIR)]
+        for u in range(PACK // PAIR):
+            for g in range(I // GATHER):
+                nc.scalar.activation(
+                    tvs[u][:, :, g * GATHER : (g + 1) * GATHER], v_banks[PAIR * u + g][:], TANH
+                )
         for t in range(PACK):
-            tv = sb(f"tv{t}", [P, I], F32)
-            tvs.append(tv)
-            nc.scalar.activation(tv[:], v_banks[t][:], TANH)
-        for t in range(PACK):
-            factor = gain_sb[:, t : t + 1]
-            if t < PAIR:
-                nc.vector.tensor_scalar(tv_gain[:, t, :], tvs[t][:], factor, None, MULT)
+            tv, factor = tvs[t // PAIR][:, t % PAIR, :], gain_sb[:, t : t + 1]
+            if t + 1 < PACK:
+                nc.scalar.activation(tv_gain[:, t, :], tv, COPY, scale=factor)
             else:
-                nc.scalar.activation(tv_gain[:, t, :], tvs[t][:], COPY, scale=factor)
+                nc.vector.tensor_scalar(tv_gain[:, t, :], tv, factor, None, MULT)
 
         ques_picked = []
         for g in range(I // GATHER):

@@ -34,7 +34,7 @@ SHARED = {
     "wq_raw": 256, "ques_scale_table": 8192, "wi0_codes0": 8448, "ques_table": 9472,
     "wo_grouped0": 10240, "x_all": 7168, "wo_grouped1": 11264,
     "wq_grouped0": 18432, "ques_picked0": 18432,
-    "wi1_raw": 26624, "wo_raw": 26624, "img_scale_table": 33792, "img_table1": 34816, "wi1_codes1": 34816,
+    "wi1_raw": 26624, "wo_raw": 26624, "img_scale_table": 34816, "img_table1": 34816, "wi1_codes1": 34816,
     "tv1": 43008, "tanh_z": 43008,
 
 }
@@ -59,12 +59,12 @@ def tile_attend_bilinearfuse_kernel(
 
         img_scale_table = sb("img_scale_table", [P, U], U8)
         ques_scale_table = sb("ques_scale_table", [P, T], U8)
-        nc.vector.memset(img_scale_table[QUAD : 2 * QUAD, :].bitcast(I32), 0)
-        nc.vector.memset(img_scale_table[2 * QUAD : P, :].bitcast(I32), 0)
+        nc.vector.memset(img_scale_table[:].bitcast(I32), 0)
         nc.vector.memset(ques_scale_table[:].bitcast(I32), 0)
-        img_planes = [sb(f"img_plane{z}", [P, I], U8) for z in range(2)]
+        both_planes = sb("img_planes", [P, 2 * I], U8)
+        img_planes = [both_planes[:, z * I : (z + 1) * I] for z in range(2)]
         ques_plane = sb("ques_plane", [P, I], U8)
-        for plane in img_planes + [ques_plane]:
+        for plane in (both_planes, ques_plane):
             nc.vector.memset(plane[:].bitcast(I32), 0)
 
         def load_rows(name, rows):
@@ -78,17 +78,18 @@ def tile_attend_bilinearfuse_kernel(
             return table
 
         nc.sync.dma_start(img_list[:], offs2)
-        nc.sync.dma_start(
-            out=img_scale_table[0:QUAD, :].bitcast(I32),
-            in_=img_scales.rearrange("z q c -> (z q) c").bitcast(I32),
-        )
         img_tables = [load_img_table(0)]
+        nc.sync.dma_start(
+            out=img_scale_table[0:P:4, :].bitcast(I32),
+            in_=img_scales.rearrange("z q c -> q z c").bitcast(I32),
+        )
         wi_raw = [load_rows("wi0_raw", wi[0:K_PASS, :])]
         nc.sync.dma_start(
             out=ques_scale_table[SPREAD_ROW:P:SPREAD, :].bitcast(I32),
             in_=ques_scales[0].bitcast(I32),
         )
         nc.sync.dma_start(ques_list[:], offs)
+        wi_raw.append(load_rows("wi1_raw", wi[K_PASS : 2 * K_PASS, :]))
         gain_sb = sb("gain_sb", [P, PACK], F32)
         nc.gpsimd.dma_start(out=gain_sb[:], in_=gain.rearrange("(p t) o -> p (t o)", t=PACK))
 
@@ -113,20 +114,14 @@ def tile_attend_bilinearfuse_kernel(
             nc.vector.tensor_copy(picked[:], window.indirect(offsets))
             return picked
 
-        img_rows = gather("img_rows", img_scale_table[:], img_list[:], I, U8)
         img_picked = [gather("img_picked0", img_tables[0][:], img_list[:], I, U16)]
+        img_rows = gather("img_rows", img_scale_table[:], img_list[:], I, U8)
 
-        def lay_img_plane(z):
-            for q in range(4):
-                first = PASS_ROW * z + 4 * q
-                nc.sync.dma_start(
-                    out=img_planes[z][QUAD * q : QUAD * q + 4, :].bitcast(I32),
-                    in_=img_rows[first : first + 4, :].bitcast(I32),
-                )
-
-        lay_img_plane(0)
-        wi_raw.append(load_rows("wi1_raw", wi[K_PASS : 2 * K_PASS, :]))
-        lay_img_plane(1)
+        for q in range(4):
+            nc.sync.dma_start(
+                out=both_planes[QUAD * q : QUAD * q + 4, :].bitcast(I32).rearrange("p (z c) -> p z c", z=2),
+                in_=img_rows[QUAD * q : QUAD * (q + 1) : 4, :].bitcast(I32),
+            )
         img_tables.append(load_img_table(1))
 
         v_banks = [
@@ -193,7 +188,7 @@ def tile_attend_bilinearfuse_kernel(
                 lhsT=codes,
                 lhsT_scale=plane,
                 rhs=img_picked[1][:].bitcast(FP4X4),
-                rhs_scale=img_planes[1][:],
+                rhs_scale=img_planes[1],
                 start=True,
                 stop=True,
             )

@@ -77,8 +77,8 @@ def tile_attend_bilinearfuse_kernel(
             nc.sync.dma_start(out=table[:].bitcast(I32), in_=img_words[z].bitcast(I32))
             return table
 
-        nc.sync.dma_start(img_list[:], offs2)
         img_tables = [load_img_table(0)]
+        nc.sync.dma_start(img_list[:], offs2)
         nc.sync.dma_start(
             out=img_scale_table[0:P:4, :].bitcast(I32),
             in_=img_scales.rearrange("z q c -> q z c").bitcast(I32),
@@ -91,7 +91,7 @@ def tile_attend_bilinearfuse_kernel(
         nc.sync.dma_start(ques_list[:], offs)
         wi_raw.append(load_rows("wi1_raw", wi[K_PASS : 2 * K_PASS, :]))
         gain_sb = sb("gain_sb", [P, PACK], F32)
-        nc.gpsimd.dma_start(out=gain_sb[:], in_=gain.rearrange("(p t) o -> p (t o)", t=PACK))
+        nc.sync.dma_start(out=gain_sb[:], in_=gain.rearrange("(p t) o -> p (t o)", t=PACK))
 
         def deal(name, raw, shares):
             halves = [sb(f"{name}_grouped{u}", [P, PAIR, P, PACK], BF16) for u in range(PACK // PAIR)]
@@ -273,7 +273,15 @@ def tile_attend_bilinearfuse_kernel(
             )
 
         def score(c, x):
-            x_codes, x_plane = quantise(f"x_{c}", x.rearrange("p i t -> p (i t)"), CHUNK)
+            x_codes = sb(f"x_codes{c}", [P, CHUNK], U32)
+            x_plane = sb(f"x_plane{c}", [P, CHUNK], U8)
+            step = CHUNK if c + 1 < CHUNKS else half
+            for lo in range(0, CHUNK, step):
+                nc.vector.quantize_mx(
+                    out=x_codes[:, lo : lo + step].bitcast(FP8X4),
+                    scales=x_plane[:, lo : lo + step],
+                    in_=x[:, lo : lo + step, :].rearrange("p i t -> p (i t)"),
+                )
             pairs = slice(c * CHUNK, (c + 1) * CHUNK)
             if c + 1 < CHUNKS:
                 bank = psum.tile([P, M // P, CHUNK], F32, name=f"out_bank{c}", tag=f"bank{c + 1}")
@@ -283,13 +291,12 @@ def tile_attend_bilinearfuse_kernel(
                 nc.scalar.copy(out=result[:], in_=bank[:])
                 nc.sync.dma_start(out=out_view[:, :, pairs], in_=result[:])
             else:
-                ways = [(nc.vector.tensor_copy, nc.sync), (nc.scalar.copy, nc.sync)]
-                for h, (copy_out, queue) in enumerate(ways):
+                result = sb("last_result", [P, M // P, CHUNK], F32)
+                for h, copy_out in enumerate((on_vector, on_scalar)):
                     bank = psum.tile([P, CHUNK], F32, name=f"last_bank{h}", tag=f"bank{z_tags[h]}")
                     answer(bank[:], h, x_codes, x_plane)
-                    result = sb(f"last_result{h}", [P, CHUNK], F32)
-                    copy_out(out=result[:], in_=bank[:])
-                    queue.dma_start(out=out_view[:, h, pairs], in_=result[:])
+                    copy_out(out=result[:, h, :], in_=bank[:])
+                nc.sync.dma_start(out=out_view[:, :, pairs], in_=result[:])
 
         x_all = sb("x_all", [P, I * PACK], BF16)
         xs = [

@@ -153,16 +153,16 @@ def tile_attend_bilinearfuse_kernel(
 
         ques_spread = gather("ques_spread", ques_scale_table[:], ques_list[:], I, U8)
         wq_raw = load_rows("wq_raw", wq)
-        ques_table = sb("ques_table", [P, T], U32)
-        nc.sync.dma_start(
-            out=ques_table[:].bitcast(I32),
-            in_=ques_words[0].rearrange("p n t -> p (n t)").bitcast(I32),
-        )
         for r in range(4):
             nc.sync.dma_start(
                 out=ques_plane[r:P:QUAD, :].bitcast(I32),
                 in_=ques_spread[SPREAD_ROW + SPREAD * r : P : QUAD, :].bitcast(I32),
             )
+        ques_table = sb("ques_table", [P, T], U32)
+        nc.sync.dma_start(
+            out=ques_table[:].bitcast(I32),
+            in_=ques_words[0].rearrange("p n t -> p (n t)").bitcast(I32),
+        )
         dealt = deal("wi0", wi_raw[0], [(on_scalar, 0, 0, P), (on_scalar, 1, 0, 40), (on_vector, 1, 40, P)])
         for u in range(PACK // PAIR):
             image_passes(0, u, quantise(f"wi0_{u}", dealt[u], PAIR * P))

@@ -32,9 +32,8 @@ PAIR = 2
 WARM_PASSES = 2
 SHARED = {
     "wq_raw": 256, "ques_scale_table": 8192, "wi0_codes0": 8448, "ques_table": 9472,
-    "wo_grouped0": 10240, "x_all": 7168, "wo_grouped1": 11264,
-    "wq_grouped0": 18432, "ques_picked0": 18432,
-    "wi1_raw": 26624, "wo_raw": 26624, "img_scale_table": 34816, "img_table1": 34816, "wi1_codes1": 34816,
+        "wq_grouped0": 18432, "ques_picked0": 18432,
+    "wi1_raw": 26624, "wo_raw": 26624, "x_all": 26624, "img_scale_table": 34816, "img_table1": 34816, "wi1_codes1": 34816,
     "tv1": 43008, "tanh_z": 43008,
 
 }
@@ -220,10 +219,8 @@ def tile_attend_bilinearfuse_kernel(
                 in_=wo_raw[:, :, h * P : (h + 1) * P].rearrange("p j (c e) -> p c j e", e=4),
             )
             wo_halves.append(grouped)
-        wo_halves = [
-            quantise(f"wo_{h}", grouped[:].rearrange("p m j -> p (m j)"), P)
-            for h, grouped in enumerate(wo_halves)
-        ]
+        wo_values = [grouped[:].rearrange("p m j -> p (m j)") for grouped in wo_halves]
+        wo_halves = [quantise("wo_0", wo_values[0], P)]
 
         half = CHUNK // 2
         pieces = [(0, half), (half, CHUNK)] + [(c * CHUNK, (c + 1) * CHUNK) for c in range(1, CHUNKS)]
@@ -305,6 +302,7 @@ def tile_attend_bilinearfuse_kernel(
         ]
         last = CHUNKS - 1
         product(0, half)
+        wo_halves.append(quantise("wo_1", wo_values[1], P))
         product(half, CHUNK)
         for c in range(1, last):
             product(c * CHUNK, (c + 1) * CHUNK)

@@ -29,11 +29,11 @@ SPREAD_ROW = 4
 SPREAD = 8
 PASS_ROW = 16
 PAIR = 2
-WARM_PASSES = 2
 SHARED = {
-    "wq_raw": 256, "ques_scale_table": 8192, "wi0_codes0": 8448, "ques_table": 9472,
+    "ques_scale_table": 8192, "ques_table": 9472,
+    "wq_raw": 57344, "img_scale_table": 65472, "img_table1": 66560, "wi1_codes1": 66560,
         "wq_grouped0": 18432, "ques_picked0": 18432,
-    "wi1_raw": 26624, "wo_raw": 26624, "x_all": 26624, "img_scale_table": 34816, "img_table1": 34816, "wi1_codes1": 34816,
+    "wi1_raw": 26624, "wo_raw": 26624, "x_all": 26624,
     "tv1": 43008, "tanh_z": 43008,
 
 }
@@ -58,8 +58,9 @@ def tile_attend_bilinearfuse_kernel(
 
         img_scale_table = sb("img_scale_table", [P, U], U8)
         ques_scale_table = sb("ques_scale_table", [P, T], U8)
-        nc.vector.memset(img_scale_table[:].bitcast(I32), 0)
         nc.vector.memset(ques_scale_table[:].bitcast(I32), 0)
+        nc.vector.memset(img_scale_table[QUAD : 2 * QUAD, :].bitcast(I32), 0)
+        nc.vector.memset(img_scale_table[2 * QUAD : P, :].bitcast(I32), 0)
         both_planes = sb("img_planes", [P, 2 * I], U8)
         img_planes = [both_planes[:, z * I : (z + 1) * I] for z in range(2)]
         ques_plane = sb("ques_plane", [P, I], U8)
@@ -76,12 +77,12 @@ def tile_attend_bilinearfuse_kernel(
             nc.sync.dma_start(out=table[:].bitcast(I32), in_=img_words[z].bitcast(I32))
             return table
 
-        img_tables = [load_img_table(0)]
-        nc.sync.dma_start(img_list[:], offs2)
         nc.sync.dma_start(
-            out=img_scale_table[0:P:4, :].bitcast(I32),
+            out=img_scale_table[0:QUAD, :].bitcast(I32),
             in_=img_scales.rearrange("z q c -> q z c").bitcast(I32),
         )
+        nc.sync.dma_start(img_list[:], offs2)
+        img_tables = [load_img_table(0)]
         wi_raw = [load_rows("wi0_raw", wi[0:K_PASS, :])]
         nc.sync.dma_start(
             out=ques_scale_table[SPREAD_ROW:P:SPREAD, :].bitcast(I32),
@@ -113,44 +114,44 @@ def tile_attend_bilinearfuse_kernel(
             nc.vector.tensor_copy(picked[:], window.indirect(offsets))
             return picked
 
-        img_picked = [gather("img_picked0", img_tables[0][:], img_list[:], I, U16)]
         img_rows = gather("img_rows", img_scale_table[:], img_list[:], I, U8)
+        img_picked = [gather("img_picked0", img_tables[0][:], img_list[:], I, U16)]
+        ques_spread = gather("ques_spread", ques_scale_table[:], ques_list[:], I, U8)
 
         for q in range(4):
             nc.sync.dma_start(
                 out=both_planes[QUAD * q : QUAD * q + 4, :].bitcast(I32).rearrange("p (z c) -> p z c", z=2),
-                in_=img_rows[QUAD * q : QUAD * (q + 1) : 4, :].bitcast(I32),
+                in_=img_rows[8 * q : 8 * (q + 1), :].bitcast(I32),
             )
         img_tables.append(load_img_table(1))
 
-        v_banks = [
-            psum.tile([P, PAIR, GATHER], F32, name=f"v_bank{b}", tag=f"bank{b}") for b in range(PACK)
-        ]
+        v_banks = {}
 
         def feature_tile(halves, t):
             codes, plane = halves[t // PAIR]
             cols = slice(t % PAIR * P, (t % PAIR + 1) * P)
             return codes[:, cols].bitcast(FP8X4), plane[:, cols]
 
-        def image_passes(z, u, half):
-            for g in range(I // GATHER):
-                spots = [(t, c) for t in range(PAIR) for c in range(GATHER // CHUNK)]
-                for t, c in spots:
-                    codes, plane = feature_tile([half], t)
-                    pairs = slice(g * GATHER + c * CHUNK, g * GATHER + (c + 1) * CHUNK)
-                    nc.tensor.matmul_mx(
-                        out=v_banks[PAIR * u + g][:, t, c * CHUNK : (c + 1) * CHUNK],
-                        lhsT=codes,
-                        lhsT_scale=plane,
-                        rhs=img_picked[z][:, pairs].bitcast(FP4X4),
-                        rhs_scale=img_planes[z][:, pairs],
-                        start=(z == 0 and (t, c) == spots[0]),
-                        stop=(z == 1 and (t, c) == spots[-1]),
-                    )
+        def image_pass(z, u, g, half):
+            if z == 0:
+                number = min(PAIR * u + g, PACK - 2)
+                v_banks[u, g] = psum.tile([P, PAIR, GATHER], F32, name=f"v_bank{u}{g}", tag=f"bank{number}")
+            spots = [(t, c) for t in range(PAIR) for c in range(GATHER // CHUNK)]
+            for t, c in spots:
+                codes, plane = feature_tile([half], t)
+                pairs = slice(g * GATHER + c * CHUNK, g * GATHER + (c + 1) * CHUNK)
+                nc.tensor.matmul_mx(
+                    out=v_banks[u, g][:, t, c * CHUNK : (c + 1) * CHUNK],
+                    lhsT=codes,
+                    lhsT_scale=plane,
+                    rhs=img_picked[z][:, pairs].bitcast(FP4X4),
+                    rhs_scale=img_planes[z][:, pairs],
+                    start=(z == 0 and (t, c) == spots[0]),
+                    stop=(z == 1 and (t, c) == spots[-1]),
+                )
 
         on_scalar, on_vector = nc.scalar.copy, nc.vector.tensor_copy
 
-        ques_spread = gather("ques_spread", ques_scale_table[:], ques_list[:], I, U8)
         wq_raw = load_rows("wq_raw", wq)
         for r in range(4):
             nc.sync.dma_start(
@@ -162,9 +163,11 @@ def tile_attend_bilinearfuse_kernel(
             out=ques_table[:].bitcast(I32),
             in_=ques_words[0].rearrange("p n t -> p (n t)").bitcast(I32),
         )
-        dealt = deal("wi0", wi_raw[0], [(on_scalar, 0, 0, P), (on_scalar, 1, 0, 40), (on_vector, 1, 40, P)])
-        for u in range(PACK // PAIR):
-            image_passes(0, u, quantise(f"wi0_{u}", dealt[u], PAIR * P))
+        dealt = deal("wi0", wi_raw[0], [(on_scalar, 0, 0, P), (on_scalar, 1, 0, P)])
+        wi0_halves = [quantise(f"wi0_{u}", dealt[u], PAIR * P) for u in range(PACK // PAIR)]
+        parts = [(u, g) for u in range(PACK // PAIR) for g in range(I // GATHER)]
+        for u, g in parts[:-1]:
+            image_pass(0, u, g, wi0_halves[u])
         dealt = deal("wi1", wi_raw[1], [(on_vector, 0, 0, P), (on_scalar, 1, 0, P)])
         wi1_first = quantise("wi1_0", dealt[0], PAIR * P)
         img_picked.append(sb("img_picked1", [P, I], U16))
@@ -174,36 +177,27 @@ def tile_attend_bilinearfuse_kernel(
                 img_tables[1][:].indirect(img_list[:, g * GATHER // 16 : (g + 1) * GATHER // 16]),
             )
         wo_raw = load_rows("wo_raw", wo)
-        image_passes(1, 0, wi1_first)
-        image_passes(1, 1, quantise("wi1_1", dealt[1], PAIR * P))
+        wi1_halves = [wi1_first, quantise("wi1_1", dealt[1], PAIR * P)]
+        tvs = [sb(f"tv{u}", [P, PAIR, I], F32) for u in range(PACK // PAIR)]
+        for u, g in parts:
+            if (u, g) == parts[-1]:
+                image_pass(0, u, g, wi0_halves[u])
+            image_pass(1, u, g, wi1_halves[u])
+            nc.scalar.activation(tvs[u][:, :, g * GATHER : (g + 1) * GATHER], v_banks[u, g][:], TANH)
 
         dealt = deal("wq", wq_raw, [(on_vector, 0, 0, P), (on_vector, 1, 0, P)])
-        wq_halves = [quantise(f"wq_{u}", dealt[u], PAIR * P) for u in range(PACK // PAIR)]
-        warm_bank = psum.tile([P, I], F32, name="warm_bank", tag=f"bank{2 * PACK - 1}")
-        for t in range(WARM_PASSES):
-            codes, plane = feature_tile(wq_halves, t)
-            nc.tensor.matmul_mx(
-                out=warm_bank[:],
-                lhsT=codes,
-                lhsT_scale=plane,
-                rhs=img_picked[1][:].bitcast(FP4X4),
-                rhs_scale=img_planes[1],
-                start=True,
-                stop=True,
-            )
         tv_gain = sb("tv_gain", [P, PACK, I], F32)
-        tvs = [sb(f"tv{u}", [P, PAIR, I], F32) for u in range(PACK // PAIR)]
-        for u in range(PACK // PAIR):
-            for g in range(I // GATHER):
+        for t in range(PAIR):
+            nc.vector.tensor_scalar(
+                tv_gain[:, t, 0:GATHER], tvs[0][:, t, 0:GATHER], gain_sb[:, t : t + 1], None, MULT
+            )
+        wq_halves = [quantise(f"wq_{u}", dealt[u], PAIR * P) for u in range(PACK // PAIR)]
+        for u, g in parts[1:]:
+            pairs = slice(g * GATHER, (g + 1) * GATHER)
+            for t in range(PAIR * u, PAIR * (u + 1)):
                 nc.scalar.activation(
-                    tvs[u][:, :, g * GATHER : (g + 1) * GATHER], v_banks[PAIR * u + g][:], TANH
+                    tv_gain[:, t, pairs], tvs[u][:, t % PAIR, pairs], COPY, scale=gain_sb[:, t : t + 1]
                 )
-        for t in range(PACK):
-            tv, factor = tvs[t // PAIR][:, t % PAIR, :], gain_sb[:, t : t + 1]
-            if t + 1 < PACK:
-                nc.scalar.activation(tv_gain[:, t, :], tv, COPY, scale=factor)
-            else:
-                nc.vector.tensor_scalar(tv_gain[:, t, :], tv, factor, None, MULT)
 
         ques_picked = []
         for g in range(I // GATHER):
@@ -224,7 +218,7 @@ def tile_attend_bilinearfuse_kernel(
 
         half = CHUNK // 2
         pieces = [(0, half), (half, CHUNK)] + [(c * CHUNK, (c + 1) * CHUNK) for c in range(1, CHUNKS)]
-        z_tags = [PACK, 0] + [PACK + c for c in range(1, CHUNKS)]
+        z_tags = [PACK, PACK - 1] + [PACK + c for c in range(1, CHUNKS)]
         tz = []
         tanh_z = sb("tanh_z", [P, PACK * I], F32)
         for n, (lo, hi) in enumerate(pieces):
@@ -281,7 +275,7 @@ def tile_attend_bilinearfuse_kernel(
                 )
             pairs = slice(c * CHUNK, (c + 1) * CHUNK)
             if c + 1 < CHUNKS:
-                bank = psum.tile([P, M // P, CHUNK], F32, name=f"out_bank{c}", tag=f"bank{c + 1}")
+                bank = psum.tile([P, M // P, CHUNK], F32, name=f"out_bank{c}", tag=f"bank{c}")
                 for h in range(M // P):
                     answer(bank[:, h, :], h, x_codes, x_plane)
                 result = sb(f"result{c}", [P, M // P, CHUNK], F32)

@@ -29,6 +29,7 @@ SPREAD_ROW = 4
 SPREAD = 8
 PASS_ROW = 16
 PAIR = 2
+WARM_WIDTHS = (256, 256, 128)
 SHARED = {
     "ques_scale_table": 8192, "ques_table": 9472,
     "wq_raw": 57344, "img_scale_table": 65472, "img_table1": 66560, "wi1_codes1": 66560,
@@ -198,6 +199,19 @@ def tile_attend_bilinearfuse_kernel(
                 nc.scalar.activation(
                     tv_gain[:, t, pairs], tvs[u][:, t % PAIR, pairs], COPY, scale=gain_sb[:, t : t + 1]
                 )
+
+        warm_bank = psum.tile([P, PAIR * P], F32, name="warm_bank", tag=f"bank{2 * PACK - 1}")
+        last_codes, last_plane = wq_halves[-1]
+        for width in WARM_WIDTHS:
+            nc.tensor.matmul_mx(
+                out=warm_bank[:, 0:width],
+                lhsT=last_codes[:, 0:P].bitcast(FP8X4),
+                lhsT_scale=last_plane[:, 0:P],
+                rhs=last_codes[:, 0:width].bitcast(FP8X4),
+                rhs_scale=last_plane[:, 0:width],
+                start=True,
+                stop=True,
+            )
 
         ques_picked = []
         for g in range(I // GATHER):

@@ -35,7 +35,7 @@ SHARED = {
     "wq_raw": 57344, "img_scale_table": 65472, "img_table1": 66560, "wi1_codes1": 66560,
         "wq_grouped0": 18432, "ques_picked0": 18432,
     "wi1_raw": 26624, "wo_raw": 26624, "x_all": 26624,
-    "tv1": 43008, "tanh_z": 43008,
+
 
 }
 
@@ -154,16 +154,16 @@ def tile_attend_bilinearfuse_kernel(
         on_scalar, on_vector = nc.scalar.copy, nc.vector.tensor_copy
 
         wq_raw = load_rows("wq_raw", wq)
-        for r in range(4):
-            nc.sync.dma_start(
-                out=ques_plane[r:P:QUAD, :].bitcast(I32),
-                in_=ques_spread[SPREAD_ROW + SPREAD * r : P : QUAD, :].bitcast(I32),
-            )
         ques_table = sb("ques_table", [P, T], U32)
         nc.sync.dma_start(
             out=ques_table[:].bitcast(I32),
             in_=ques_words[0].rearrange("p n t -> p (n t)").bitcast(I32),
         )
+        for r in range(4):
+            nc.sync.dma_start(
+                out=ques_plane[r:P:QUAD, :].bitcast(I32),
+                in_=ques_spread[SPREAD_ROW + SPREAD * r : P : QUAD, :].bitcast(I32),
+            )
         dealt = deal("wi0", wi_raw[0], [(on_scalar, 0, 0, P), (on_scalar, 1, 0, P)])
         wi0_halves = [quantise(f"wi0_{u}", dealt[u], PAIR * P) for u in range(PACK // PAIR)]
         parts = [(u, g) for u in range(PACK // PAIR) for g in range(I // GATHER)]

@@ -32,7 +32,7 @@ PAIR = 2
 WARM_WIDTHS = (256, 256, 128)
 SHARED = {
     "ques_scale_table": 8192, "ques_table": 9472,
-    "wq_raw": 57344, "img_scale_table": 65472, "img_table1": 66560, "wi1_codes1": 66560,
+    "wq_raw": 57344, "img_scale_table": 65472, "gain_sb": 65536, "img_table1": 66560, "wi1_codes1": 66560,
         "wq_grouped0": 18432, "ques_picked0": 18432,
     "wi1_raw": 26624, "wo_raw": 26624, "x_all": 26624,
 
@@ -91,8 +91,6 @@ def tile_attend_bilinearfuse_kernel(
         )
         nc.sync.dma_start(ques_list[:], offs)
         wi_raw.append(load_rows("wi1_raw", wi[K_PASS : 2 * K_PASS, :]))
-        gain_sb = sb("gain_sb", [P, PACK], F32)
-        nc.sync.dma_start(out=gain_sb[:], in_=gain.rearrange("(p t) o -> p (t o)", t=PACK))
 
         def deal(name, raw, shares):
             halves = [sb(f"{name}_grouped{u}", [P, PAIR, P, PACK], BF16) for u in range(PACK // PAIR)]
@@ -154,6 +152,8 @@ def tile_attend_bilinearfuse_kernel(
         on_scalar, on_vector = nc.scalar.copy, nc.vector.tensor_copy
 
         wq_raw = load_rows("wq_raw", wq)
+        gain_sb = sb("gain_sb", [P, PACK], F32)
+        nc.sync.dma_start(out=gain_sb[:], in_=gain.rearrange("(p t) o -> p (t o)", t=PACK))
         ques_table = sb("ques_table", [P, T], U32)
         nc.sync.dma_start(
             out=ques_table[:].bitcast(I32),
@@ -188,12 +188,11 @@ def tile_attend_bilinearfuse_kernel(
 
         dealt = deal("wq", wq_raw, [(on_vector, 0, 0, P), (on_vector, 1, 0, P)])
         tv_gain = sb("tv_gain", [P, PACK, I], F32)
+        wq_halves = [quantise("wq_0", dealt[0], PAIR * P)]
         for t in range(PAIR):
-            nc.vector.tensor_scalar(
-                tv_gain[:, t, 0:GATHER], tvs[0][:, t, 0:GATHER], gain_sb[:, t : t + 1], None, MULT
-            )
-        wq_halves = [quantise(f"wq_{u}", dealt[u], PAIR * P) for u in range(PACK // PAIR)]
-        for u, g in parts[1:]:
+            nc.vector.tensor_scalar(tv_gain[:, t, :], tvs[0][:, t, :], gain_sb[:, t : t + 1], None, MULT)
+        wq_halves.append(quantise("wq_1", dealt[1], PAIR * P))
+        for u, g in parts[PAIR:]:
             pairs = slice(g * GATHER, (g + 1) * GATHER)
             for t in range(PAIR * u, PAIR * (u + 1)):
                 nc.scalar.activation(

@@ -131,22 +131,21 @@ def tile_attend_bilinearfuse_kernel(
             cols = slice(t % PAIR * P, (t % PAIR + 1) * P)
             return codes[:, cols].bitcast(FP8X4), plane[:, cols]
 
-        def image_pass(z, u, g, half):
+        def image_pass(z, part, half):
+            u, lo, hi, number = part
             if z == 0:
-                number = min(PAIR * u + g, PACK - 2)
-                v_banks[u, g] = psum.tile([P, PAIR, GATHER], F32, name=f"v_bank{u}{g}", tag=f"bank{number}")
-            spots = [(t, c) for t in range(PAIR) for c in range(GATHER // CHUNK)]
-            for t, c in spots:
+                v_banks[part] = psum.tile([P, PAIR, hi - lo], F32, name=f"v_bank{u}_{lo}", tag=f"bank{number}")
+            spots = [(t, first) for t in range(PAIR) for first in range(lo, hi, CHUNK)]
+            for t, first in spots:
                 codes, plane = feature_tile([half], t)
-                pairs = slice(g * GATHER + c * CHUNK, g * GATHER + (c + 1) * CHUNK)
                 nc.tensor.matmul_mx(
-                    out=v_banks[u, g][:, t, c * CHUNK : (c + 1) * CHUNK],
+                    out=v_banks[part][:, t, first - lo : first - lo + CHUNK],
                     lhsT=codes,
                     lhsT_scale=plane,
-                    rhs=img_picked[z][:, pairs].bitcast(FP4X4),
-                    rhs_scale=img_planes[z][:, pairs],
-                    start=(z == 0 and (t, c) == spots[0]),
-                    stop=(z == 1 and (t, c) == spots[-1]),
+                    rhs=img_picked[z][:, first : first + CHUNK].bitcast(FP4X4),
+                    rhs_scale=img_planes[z][:, first : first + CHUNK],
+                    start=(z == 0 and (t, first) == spots[0]),
+                    stop=(z == 1 and (t, first) == spots[-1]),
                 )
 
         on_scalar, on_vector = nc.scalar.copy, nc.vector.tensor_copy
@@ -166,9 +165,9 @@ def tile_attend_bilinearfuse_kernel(
             )
         dealt = deal("wi0", wi_raw[0], [(on_scalar, 0, 0, P), (on_scalar, 1, 0, P)])
         wi0_halves = [quantise(f"wi0_{u}", dealt[u], PAIR * P) for u in range(PACK // PAIR)]
-        parts = [(u, g) for u in range(PACK // PAIR) for g in range(I // GATHER)]
-        for u, g in parts[:-1]:
-            image_pass(0, u, g, wi0_halves[u])
+        parts = [(0, 0, CHUNK, 3), (0, CHUNK, GATHER, 0), (0, GATHER, I, 1), (1, 0, GATHER, 2), (1, GATHER, I, 1)]
+        for part in parts[:-1]:
+            image_pass(0, part, wi0_halves[part[0]])
         dealt = deal("wi1", wi_raw[1], [(on_vector, 0, 0, P), (on_scalar, 1, 0, P)])
         wi1_first = quantise("wi1_0", dealt[0], PAIR * P)
         img_picked.append(sb("img_picked1", [P, I], U16))
@@ -180,20 +179,23 @@ def tile_attend_bilinearfuse_kernel(
         wo_raw = load_rows("wo_raw", wo)
         wi1_halves = [wi1_first, quantise("wi1_1", dealt[1], PAIR * P)]
         tvs = [sb(f"tv{u}", [P, PAIR, I], F32) for u in range(PACK // PAIR)]
-        for u, g in parts:
-            if (u, g) == parts[-1]:
-                image_pass(0, u, g, wi0_halves[u])
-            image_pass(1, u, g, wi1_halves[u])
-            nc.scalar.activation(tvs[u][:, :, g * GATHER : (g + 1) * GATHER], v_banks[u, g][:], TANH)
+        for part in parts:
+            u, lo, hi = part[:3]
+            if part == parts[-1]:
+                image_pass(0, part, wi0_halves[u])
+            image_pass(1, part, wi1_halves[u])
+            nc.scalar.activation(tvs[u][:, :, lo:hi], v_banks[part][:], TANH)
 
         dealt = deal("wq", wq_raw, [(on_vector, 0, 0, P), (on_vector, 1, 0, P)])
         tv_gain = sb("tv_gain", [P, PACK, I], F32)
         wq_halves = [quantise("wq_0", dealt[0], PAIR * P)]
         for t in range(PAIR):
-            nc.vector.tensor_scalar(tv_gain[:, t, :], tvs[0][:, t, :], gain_sb[:, t : t + 1], None, MULT)
+            pairs = slice(t * GATHER, I)
+            nc.vector.tensor_scalar(tv_gain[:, t, pairs], tvs[0][:, t, pairs], gain_sb[:, t : t + 1], None, MULT)
         wq_halves.append(quantise("wq_1", dealt[1], PAIR * P))
-        for u, g in parts[PAIR:]:
-            pairs = slice(g * GATHER, (g + 1) * GATHER)
+        nc.scalar.activation(tv_gain[:, 1, 0:GATHER], tvs[0][:, 1, 0:GATHER], COPY, scale=gain_sb[:, 1:2])
+        for u, lo, hi, number in parts[-PAIR:]:
+            pairs = slice(lo, hi)
             for t in range(PAIR * u, PAIR * (u + 1)):
                 nc.scalar.activation(
                     tv_gain[:, t, pairs], tvs[u][:, t % PAIR, pairs], COPY, scale=gain_sb[:, t : t + 1]

from contextlib import ExitStack

import concourse.mybir as mybir

K, T, R, U, I, F, M = 512, 2048, 1024, 2048, 512, 512, 256
FLOPS = 2 * I * (K * F + R * F + F * M)

F32 = mybir.dt.float32
BF16 = mybir.dt.bfloat16
I32 = mybir.dt.int32
U32 = mybir.dt.uint32
U16 = mybir.dt.uint16
U8 = mybir.dt.uint8
FP8X4 = mybir.dt.float8_e4m3fn_x4
FP4X4 = mybir.dt.float4_e2m1fn_x4
TANH = mybir.ActivationFunctionType.Tanh
COPY = mybir.ActivationFunctionType.Copy
ADD = mybir.AluOpType.add
MULT = mybir.AluOpType.mult

P = 128
PACK = 4
K_PASS = P * PACK
QUAD = 32
CHUNK = 128
CHUNKS = I // CHUNK
GATHER = 256
SPREAD_ROW = 4
SPREAD = 8
PASS_ROW = 16
PAIR = 2
WARM_WIDTHS = (256, 256, 128)
SHARED = {
    "ques_scale_table": 8192, "ques_table": 9472,
    "wq_raw": 57344, "img_scale_table": 65472, "gain_sb": 65536, "img_table1": 66560, "wi1_codes1": 66560,
        "wq_grouped0": 18432, "ques_picked0": 18432,
    "wi1_raw": 26624, "wo_raw": 26624, "x_all": 26624,


}


def tile_attend_bilinearfuse_kernel(
    tc, ques_words, ques_scales, img_words, img_scales, wq, wi, gain, wo, offs, offs2, out
):
    nc = tc.nc
    with ExitStack() as ctx:
        keep = ctx.enter_context(tc.tile_pool(name="keep", bufs=1))
        shared = ctx.enter_context(tc.tile_pool(name="shared", bufs=1))
        psum = ctx.enter_context(tc.psum_pool(name="psum", bufs=1))

        def sb(name, shape, dtype):
            if name in SHARED:
                return shared.tile(shape, dtype, name=name, offset=SHARED[name], align_bytes=64)
            return keep.tile(shape, dtype, name=name, align_bytes=64)

        ques_list = keep.tile([P, I // 16], U16, name="ques_list")
        img_list = keep.tile([P, I // 16], U16, name="img_list")

        img_scale_table = sb("img_scale_table", [P, U], U8)
        ques_scale_table = sb("ques_scale_table", [P, T], U8)
        nc.vector.memset(ques_scale_table[:].bitcast(I32), 0)
        nc.vector.memset(img_scale_table[QUAD : 2 * QUAD, :].bitcast(I32), 0)
        nc.vector.memset(img_scale_table[2 * QUAD : P, :].bitcast(I32), 0)
        both_planes = sb("img_planes", [P, 2 * I], U8)
        img_planes = [both_planes[:, z * I : (z + 1) * I] for z in range(2)]
        ques_plane = sb("ques_plane", [P, I], U8)
        for plane in (both_planes, ques_plane):
            nc.vector.memset(plane[:].bitcast(I32), 0)

        def load_rows(name, rows):
            raw = sb(name, [P, PACK, rows.shape[1]], F32)
            nc.sync.dma_start(out=raw[:], in_=rows.rearrange("(p j) c -> p j c", j=PACK))
            return raw

        def load_img_table(z):
            table = sb(f"img_table{z}", [P, U], U16)
            nc.sync.dma_start(out=table[:].bitcast(I32), in_=img_words[z].bitcast(I32))
            return table

        nc.sync.dma_start(
            out=img_scale_table[0:QUAD, :].bitcast(I32),
            in_=img_scales.rearrange("z q c -> q z c").bitcast(I32),
        )
        nc.sync.dma_start(img_list[:], offs2)
        img_tables = [load_img_table(0)]
        wi_raw = [load_rows("wi0_raw", wi[0:K_PASS, :])]
        nc.sync.dma_start(
            out=ques_scale_table[SPREAD_ROW:P:SPREAD, :].bitcast(I32),
            in_=ques_scales[0].bitcast(I32),
        )
        nc.sync.dma_start(ques_list[:], offs)
        wi_raw.append(load_rows("wi1_raw", wi[K_PASS : 2 * K_PASS, :]))

        def deal(name, raw, shares):
            halves = [sb(f"{name}_grouped{u}", [P, PAIR, P, PACK], BF16) for u in range(PACK // PAIR)]
            for copy_part, u, lo, hi in shares:
                copy_part(
                    out=halves[u][:, :, lo:hi, :].rearrange("p t m j -> p m j t"),
                    in_=raw[:]
                    .rearrange("p j (m t) -> p m j t", t=PACK)[:, lo:hi, :, u * PAIR : (u + 1) * PAIR],
                )
            return [half[:].rearrange("p t m j -> p (t m j)") for half in halves]

        def quantise(name, values, width):
            codes = sb(name.replace("_", "_codes"), [P, width], U32)
            plane = sb(name.replace("_", "_plane"), [P, width], U8)
            nc.vector.quantize_mx(out=codes[:].bitcast(FP8X4), scales=plane[:], in_=values)
            return codes, plane

        def gather(name, window, offsets, width, dtype):
            picked = sb(name, [P, width], dtype)
            nc.vector.tensor_copy(picked[:], window.indirect(offsets))
            return picked

        img_rows = gather("img_rows", img_scale_table[:], img_list[:], I, U8)
        img_picked = [gather("img_picked0", img_tables[0][:], img_list[:], I, U16)]
        ques_spread = gather("ques_spread", ques_scale_table[:], ques_list[:], I, U8)

        for q in range(4):
            nc.sync.dma_start(
                out=both_planes[QUAD * q : QUAD * q + 4, :].bitcast(I32).rearrange("p (z c) -> p z c", z=2),
                in_=img_rows[8 * q : 8 * (q + 1), :].bitcast(I32),
            )
        img_tables.append(load_img_table(1))

        v_banks = {}

        def feature_tile(halves, t):
            codes, plane = halves[t // PAIR]
            cols = slice(t % PAIR * P, (t % PAIR + 1) * P)
            return codes[:, cols].bitcast(FP8X4), plane[:, cols]

        def image_pass(z, part, half):
            u, lo, hi, number = part
            if z == 0:
                v_banks[part] = psum.tile([P, PAIR, hi - lo], F32, name=f"v_bank{u}_{lo}", tag=f"bank{number}")
            spots = [(t, first) for t in range(PAIR) for first in range(lo, hi, CHUNK)]
            for t, first in spots:
                codes, plane = feature_tile([half], t)
                nc.tensor.matmul_mx(
                    out=v_banks[part][:, t, first - lo : first - lo + CHUNK],
                    lhsT=codes,
                    lhsT_scale=plane,
                    rhs=img_picked[z][:, first : first + CHUNK].bitcast(FP4X4),
                    rhs_scale=img_planes[z][:, first : first + CHUNK],
                    start=(z == 0 and (t, first) == spots[0]),
                    stop=(z == 1 and (t, first) == spots[-1]),
                )

        on_scalar, on_vector = nc.scalar.copy, nc.vector.tensor_copy

        wq_raw = load_rows("wq_raw", wq)
        gain_sb = sb("gain_sb", [P, PACK], F32)
        nc.sync.dma_start(out=gain_sb[:], in_=gain.rearrange("(p t) o -> p (t o)", t=PACK))
        ques_table = sb("ques_table", [P, T], U32)
        nc.sync.dma_start(
            out=ques_table[:].bitcast(I32),
            in_=ques_words[0].rearrange("p n t -> p (n t)").bitcast(I32),
        )
        for r in range(4):
            nc.sync.dma_start(
                out=ques_plane[r:P:QUAD, :].bitcast(I32),
                in_=ques_spread[SPREAD_ROW + SPREAD * r : P : QUAD, :].bitcast(I32),
            )
        dealt = deal("wi0", wi_raw[0], [(on_scalar, 0, 0, P), (on_scalar, 1, 0, P)])
        wi0_halves = [quantise(f"wi0_{u}", dealt[u], PAIR * P) for u in range(PACK // PAIR)]
        parts = [(0, 0, CHUNK, 3), (0, CHUNK, GATHER, 0), (0, GATHER, I, 1), (1, 0, GATHER, 2), (1, GATHER, I, 1)]
        for part in parts[:-1]:
            image_pass(0, part, wi0_halves[part[0]])
        dealt = deal("wi1", wi_raw[1], [(on_vector, 0, 0, P), (on_scalar, 1, 0, P)])
        wi1_first = quantise("wi1_0", dealt[0], PAIR * P)
        img_picked.append(sb("img_picked1", [P, I], U16))
        for g in range(I // GATHER):
            nc.vector.tensor_copy(
                img_picked[1][:, g * GATHER : (g + 1) * GATHER],
                img_tables[1][:].indirect(img_list[:, g * GATHER // 16 : (g + 1) * GATHER // 16]),
            )
        wo_raw = load_rows("wo_raw", wo)
        wi1_halves = [wi1_first, quantise("wi1_1", dealt[1], PAIR * P)]
        tvs = [sb(f"tv{u}", [P, PAIR, I], F32) for u in range(PACK // PAIR)]
        for part in parts:
            u, lo, hi = part[:3]
            if part == parts[-1]:
                image_pass(0, part, wi0_halves[u])
            image_pass(1, part, wi1_halves[u])
            nc.scalar.activation(tvs[u][:, :, lo:hi], v_banks[part][:], TANH)

        dealt = deal("wq", wq_raw, [(on_vector, 0, 0, P), (on_vector, 1, 0, P)])
        tv_gain = sb("tv_gain", [P, PACK, I], F32)
        wq_halves = [quantise("wq_0", dealt[0], PAIR * P)]
        for t in range(PAIR):
            pairs = slice(t * GATHER, I)
            nc.vector.tensor_scalar(tv_gain[:, t, pairs], tvs[0][:, t, pairs], gain_sb[:, t : t + 1], None, MULT)
        wq_halves.append(quantise("wq_1", dealt[1], PAIR * P))
        nc.scalar.activation(tv_gain[:, 1, 0:GATHER], tvs[0][:, 1, 0:GATHER], COPY, scale=gain_sb[:, 1:2])
        for u, lo, hi, number in parts[-PAIR:]:
            pairs = slice(lo, hi)
            for t in range(PAIR * u, PAIR * (u + 1)):
                nc.scalar.activation(
                    tv_gain[:, t, pairs], tvs[u][:, t % PAIR, pairs], COPY, scale=gain_sb[:, t : t + 1]
                )

        warm_bank = psum.tile([P, PAIR * P], F32, name="warm_bank", tag=f"bank{2 * PACK - 1}")
        last_codes, last_plane = wq_halves[-1]
        for width in WARM_WIDTHS:
            nc.tensor.matmul_mx(
                out=warm_bank[:, 0:width],
                lhsT=last_codes[:, 0:P].bitcast(FP8X4),
                lhsT_scale=last_plane[:, 0:P],
                rhs=last_codes[:, 0:width].bitcast(FP8X4),
                rhs_scale=last_plane[:, 0:width],
                start=True,
                stop=True,
            )

        ques_picked = []
        for g in range(I // GATHER):
            columns = slice(g * GATHER // 16, (g + 1) * GATHER // 16)
            ques_picked.append(
                gather(f"ques_picked{g}", ques_table[:], ques_list[:, columns], GATHER, U32)
            )
        wo_halves = []
        for h in range(M // P):
            grouped = sb(f"wo_grouped{h}", [P, P, PACK], BF16)
            nc.vector.tensor_copy(
                out=grouped[:].rearrange("p (c e) j -> p c j e", e=4),
                in_=wo_raw[:, :, h * P : (h + 1) * P].rearrange("p j (c e) -> p c j e", e=4),
            )
            wo_halves.append(grouped)
        wo_values = [grouped[:].rearrange("p m j -> p (m j)") for grouped in wo_halves]
        wo_halves = [quantise("wo_0", wo_values[0], P)]

        half = CHUNK // 2
        pieces = [(0, half), (half, CHUNK)] + [(c * CHUNK, (c + 1) * CHUNK) for c in range(1, CHUNKS)]
        z_tags = [PACK, PACK - 1] + [PACK + c for c in range(1, CHUNKS)]
        tz = []
        tanh_z = sb("tanh_z", [P, PACK * I], F32)
        for n, (lo, hi) in enumerate(pieces):
            bank = psum.tile([P, PACK, hi - lo], F32, name=f"z_bank{n}", tag=f"bank{z_tags[n]}")
            g, first = divmod(lo, GATHER)
            for t in range(PACK):
                codes, plane = feature_tile(wq_halves, t)
                nc.tensor.matmul_mx(
                    out=bank[:, t, :],
                    lhsT=codes,
                    lhsT_scale=plane,
                    rhs=ques_picked[g][:, first : first + hi - lo].bitcast(FP8X4),
                    rhs_scale=ques_plane[:, lo:hi],
                    start=True,
                    stop=True,
                )
            piece = tanh_z[:, PACK * lo : PACK * hi]
            nc.scalar.activation(piece, bank[:].rearrange("p t i -> p (t i)"), TANH)
            tz.append(piece.rearrange("p (t i) -> p t i", t=PACK))

        out_view = out.rearrange("(h p) i -> p h i", p=P)

        def product(lo, hi):
            n = max(k for k, piece in enumerate(pieces) if piece[0] <= lo)
            c, first = divmod(lo, CHUNK)
            nc.vector.tensor_tensor(
                xs[c][:, first : first + hi - lo, :].rearrange("p (c e) t -> p c t e", e=2),
                tz[n][:, :, lo - pieces[n][0] : hi - pieces[n][0]].rearrange("p t (c e) -> p c t e", e=2),
                tv_gain[:, :, lo:hi].rearrange("p t (c e) -> p c t e", e=2),
                MULT,
            )

        def answer(bank, h, x_codes, x_plane):
            codes, plane = wo_halves[h]
            nc.tensor.matmul_mx(
                out=bank,
                lhsT=codes[:].bitcast(FP8X4),
                lhsT_scale=plane[:],
                rhs=x_codes[:].bitcast(FP8X4),
                rhs_scale=x_plane[:],
                start=True,
                stop=True,
            )

        def score(c, x):
            x_codes = sb(f"x_codes{c}", [P, CHUNK], U32)
            x_plane = sb(f"x_plane{c}", [P, CHUNK], U8)
            step = CHUNK if c + 1 < CHUNKS else half
            for lo in range(0, CHUNK, step):
                nc.vector.quantize_mx(
                    out=x_codes[:, lo : lo + step].bitcast(FP8X4),
                    scales=x_plane[:, lo : lo + step],
                    in_=x[:, lo : lo + step, :].rearrange("p i t -> p (i t)"),
                )
            pairs = slice(c * CHUNK, (c + 1) * CHUNK)
            if c + 1 < CHUNKS:
                bank = psum.tile([P, M // P, CHUNK], F32, name=f"out_bank{c}", tag=f"bank{c}")
                for h in range(M // P):
                    answer(bank[:, h, :], h, x_codes, x_plane)
                result = sb(f"result{c}", [P, M // P, CHUNK], F32)
                nc.scalar.copy(out=result[:], in_=bank[:])
                nc.sync.dma_start(out=out_view[:, :, pairs], in_=result[:])
            else:
                result = sb("last_result", [P, M // P, CHUNK], F32)
                for h, copy_out in enumerate((on_vector, on_scalar)):
                    bank = psum.tile([P, CHUNK], F32, name=f"last_bank{h}", tag=f"bank{z_tags[h]}")
                    answer(bank[:], h, x_codes, x_plane)
                    copy_out(out=result[:, h, :], in_=bank[:])
                nc.sync.dma_start(out=out_view[:, :, pairs], in_=result[:])

        x_all = sb("x_all", [P, I * PACK], BF16)
        xs = [
            x_all[:, c * CHUNK * PACK : (c + 1) * CHUNK * PACK].rearrange("p (i t) -> p i t", t=PACK)
            for c in range(CHUNKS)
        ]
        last = CHUNKS - 1
        product(0, half)
        wo_halves.append(quantise("wo_1", wo_values[1], P))
        product(half, CHUNK)
        for c in range(1, last):
            product(c * CHUNK, (c + 1) * CHUNK)
            score(c - 1, xs[c - 1])
        product(last * CHUNK, I - half)
        score(last - 1, xs[last - 1])
        product(I - half, I)
        score(last, xs[last])
